import numpy as np, ml_dtypes
CORES = [23,119,17,113]
N = 4
BF = ml_dtypes.bfloat16
W, L, Q, PARTS, TH, AC, T = 4096, 512, 8, 2, 96, 5, 4
S, H, LB = 512, 2048, 12
def parts(rng):
    amp = rng.choice(np.array([176, 208, 256]), (N, 8, 1, 1)); lo = ((257 - amp) * rng.random((N, 8, 1, 1))).astype(np.int64)
    x = lo + (amp * rng.random((N, 8, 16, W), dtype=np.float32)).astype(np.int64)
    return np.minimum(x, 255), rng.integers(0, W, (N, 8, 16, W)), rng.integers(0, W, (N, 8, 16, L)), rng.integers(0, 64, (N, 8, 16))
def pack(x, b, c, w):
    return {"x": x.reshape(N, 128, W).astype(np.float32).astype(BF), "pk": (b[..., :H] + W * b[..., H:]).reshape(N, 128, H).astype(np.int32),
            "cb": c.reshape(N, 128, L).astype(np.int32), "wt": w.reshape(N, 128, 1).astype(np.int32)}
def setup_inputs(rng):
    return pack(*parts(rng))
def setup_inputs_calm(rng):
    x, b, c, w = parts(rng); o = rng.permutation(8); k = np.arange(16)[:, None]
    for g in o[:3]:
        x[:, g] = int(rng.integers(0, 256 - TH)) + rng.integers(0, TH + 1, (N, 16, W))
    g = o[3]; s = rng.integers(0, 16, (N, 16, W))
    x[:, g] = np.where(np.arange(W) >= H, 255 - s, s)
    c[:, g] = rng.integers(0, H, (N, 16, L)) + H * (k % 2); b[:, g] = rng.integers(0, H, (N, 16, W)) + H * (k % 2)
    q = int(rng.integers(0, N))
    for g in o[3:]:
        x[q, g] = int(rng.integers(0, 256 - TH)) + rng.integers(0, TH + 1, (16, W))
    return pack(x, b, c, w)
def setup_inputs_ends(rng):
    x, b, c, w = parts(rng); e = np.array([0, 1, H - 1, H, W - 2, W - 1])
    c[:, 0] = rng.choice(e, (N, 16, L)); b[:, 0] = rng.choice(e, (N, 16, W))
    c[:, 1] = rng.integers(0, W, (N, 1, L)); c[:, 2] = rng.integers(0, W, (N, 16, 1))
    b[:, 3] = np.arange(W); w[:, 4] = 0; w[:, 5] = 63
    x[:, 5] = 255 * (rng.random((N, 16, W)) < 0.85); x[1::2, 5] = rng.integers(200, 256, (N // 2, 16, W))
    x[:, 6] |= 15; w[:, 7, :15] = 0; w[:, 7, 15] = rng.integers(1, 64, N)
    return pack(x, b, c, w)
def setup_inputs_heavy(rng):
    x, b, c, w = parts(rng); k = np.arange(16)[:, None]; q = int(rng.integers(0, N)); A = 15 * (L - 1)
    s = rng.integers(0, 16, (N, 8, 16, W)); x = np.where(np.arange(W) >= H, 255 - s, s)
    c = rng.integers(16, H, (N, 8, 16, L)) + H * (k % 2); b = rng.integers(16, H, (N, 8, 16, W)) + H * (k % 2)
    for g in range(8):
        p = rng.permutation(16); j = int(rng.integers(1, 15))
        if g % 4 < 2:
            hs = np.arange(227700, 240900); hs = hs[((37 * hs + A) & (2 * W - 1)) == (W, 2 * W - 1)[g % 4]]; h = int(rng.choice(hs))
            last = 192 + (h - 192) % 63; a = (h - last) // 63
            u = rng.permutation(np.repeat(np.arange(15), 15))[:a - 3600]
            val = np.insert(240 + np.bincount(u, minlength=15), j, last); w[q, g] = 63; w[q, g, j] = 1
        elif g % 4 == 2:
            val = rng.integers(0, 16, 16); val[j] = 255
        else:
            val = int(rng.integers(0, 256 - TH)) + rng.integers(0, TH + 1, 16)
        x[q, g][:, p] = val; c[q, g, :, 1 + PARTS * int(rng.integers(0, L // PARTS))] = p
    return pack(x, b, c, w)
def setup_inputs_ties(rng):
    x, b, c, w = parts(rng)
    for r in range(N):
        for g in range(0, 8, 2):
            o = rng.permutation(W); cl = np.zeros(W, np.int64); cl[o[W // 3:2 * (W // 3)]] = 1; cl[o[2 * (W // 3):]] = 2
            lo = int(rng.integers(0, 255 - TH)); x[r, g] = np.array([lo, lo + TH, lo + TH + 1])[cl][None, :]
            n = rng.choice(np.array([0, 1, AC - 1, AC, AC + 1, 15]), L)
            if r == 0 and g == 0: n[:] = AC
            if r == 0 and g == 2: n[:] = AC + 1
            cr = np.zeros((17, L), bool); cr[1:16] = np.argsort(np.argsort(rng.random((15, L)), axis=0), axis=0) < n
            s = 2 * ((np.add.accumulate(cr[:16].astype(np.int64), axis=0) + rng.integers(0, 2, L)) % 2)
            s = np.where(~cr[:16] & ~cr[1:] & (rng.random((16, L)) < 0.5), 1, s)
            for a in range(3):
                mem = np.flatnonzero(cl == a); c[r, g] = np.where(s == a, mem[rng.integers(0, mem.size, (16, L))], c[r, g])
    return pack(x, b, c, w)
def setup_inputs_spread(rng):
    x, b, c, w = parts(rng); lo = rng.choice(np.array([0.0, 5.0, 7.0]), (N, 8, 1, 1))
    x = np.minimum((np.exp2(lo + (8 - lo) * rng.random((N, 8, 1, W))) * rng.random((N, 8, 16, W))).astype(np.int64), 255)
    x = np.where(rng.random((N, 8, 1, W)) < 0.25, 255 - x, x)
    c = np.minimum((W * rng.random((N, 8, 16, L)) ** 3).astype(np.int64), W - 1); b = np.minimum((W * rng.random((N, 8, 16, W)) ** 2).astype(np.int64), W - 1)
    w = np.minimum(np.exp2(6 * rng.random((N, 8, 16))).astype(np.int64), 63)
    return pack(x, b, c, w)
def check_inputs(d):
    bad = []
    for k, hi in (("x", 255), ("pk", W * W - 1), ("cb", W - 1), ("wt", 63)):
        a = np.asarray(d[k]).astype(np.float64)
        if not np.all((a >= 0) & (a <= hi) & (a == np.floor(a))): bad.append("range of " + k)
    return bad
def reference(x, pk, cb, wt):
    X = x.astype(np.float32).astype(np.int64).reshape(N, 8, 16, W); p = pk.astype(np.int64).reshape(N, 8, 16, H)
    B = np.concatenate([p & (W - 1), p >> LB], axis=3)
    c = cb.astype(np.int64).reshape(N, 8, 16, L); w = wt.astype(np.int64).reshape(N, 8, 16, 1)
    lane = np.arange(L); rr = np.arange(N)[:, None, None, None]; gg = np.arange(8)[None, :, None, None]
    for t in range(T):
        e = np.take_along_axis(X, c, 3)
        z = np.concatenate([np.zeros((N, 8, 1, L), np.int64), e[:, :, :15] & 15], axis=2)
        v = X[rr, gg, z, c]
        cr = np.concatenate([np.zeros((N, 8, 1, L), bool), np.abs(v[:, :, 1:] - v[:, :, :15]) > TH], axis=2)
        n = np.add.reduce(cr.astype(np.int64), axis=2); A = np.add.reduce(n, axis=2)[:, :, None]; h = np.add.reduce(w * v, axis=2)
        ok = n <= AC; place = S * ((h + A) & (Q - 1)) + lane; nxt = (37 * h + A) & (W - 1)
        mend = np.where(cr, np.take_along_axis(B, c, 3), c)
        X, B = np.array(X), np.array(B)
        for r in range(N):
            for m in range(PARTS):
                q = r if m == 0 else (r + 1 + (t + m - 1) % (N - 1)) % N
                for g in range(8):
                    i = lane[m::PARTS]; i = i[ok[r, g, i]]
                    X[q, g][:, place[r, g, i]] = v[r, g][:, i]; B[q, g][:, place[r, g, i]] = c[r, g][:, i]
        new = np.take_along_axis(B, np.repeat(nxt[:, :, None, :], 16, axis=2), 3)
        c = np.where(ok[:, :, None, :], new, mend)
    return {"yx": X.reshape(N, 128, W).astype(np.float32).astype(BF), "yc": c.reshape(N, 128, L).astype(np.float32)}

@@ -1,0 +1,496 @@
+from concourse.mybir import dt, AluOpType, AxisListType, ActivationFunctionType
+
+A = AluOpType
+F = ActivationFunctionType
+ROUNDS = 4
+NB = 4
+W = 4096
+MEND = 4096
+DUMP = 4608
+WIN = DUMP + 4096
+LONG = {"f": "float32", "b": "bfloat16", "h": "float16", "i": "int32", "u": "uint16"}
+SCRATCH = {}
+_spec = """Dt:8704b Bt:8704i xin:4096b pin:2048i ci:512i wi:1i G:8192b GB:8192h VM:4096b R1:256f wT:256b Wz:256b SQ0:136f SQ1:136f
+Vt0:144b Vt1:144b VS:512b CC:512b nd:128b ad:128b BT:512h t2:512f ycs:512f Rr:1f Hs:32f na:32f na1:32f rp:32f
+i1:32i i2:32i pf:32f x1:32i x2:32i y1:32f y3:32f nx:32u pc:1i ki:1i gi:1i si:1i col:32f wb:1b J:128i Jk:128i Js:128i
+Jg:128i K8:128i S8:128i G8:128i K16:16i iL:32f mL:32f iL0:32i mL0:32i u1:128f u2:128f v1:128f v2:128f colk:16f
+BO:128b BW:128b BOf:128f BS:128b ID:128b NID:128b ID16:128h NID16:128h EK:128b DK:128h DM:128b DC:128b SX:128b
+PL:2048b LO:2048b LW:2048b"""
+for _t in range(ROUNDS):
+    _spec += " cU_%d:512u c16_%d:512h Dn_%d:512b pU_%d:32u rC_%d:256u rD_%d:256b rP_%d:16u" % ((_t,) * 7)
+for _w in _spec.split():
+    _n, _d = _w.split(":")
+    SCRATCH[_n] = ("sbuf", [128, int(_d[:-1])], LONG[_d[-1]])
+for _t in range(8):
+    SCRATCH["ps%d" % _t] = ("psum", [128, 512], "float32")
+SEMAPHORES = "qv qs qt qg loc lci lwt lx0 lx1 lx2 lx3 lp0 lp1 arr0 arr1 arr2 arr3 o0 o1 o2 o3 o4".split()
+K_, G_, S_, P_, P1, G16, G32, IS15, WSC, THR, DBI, H0, WF, K1 = range(14)
+
+
+def rank_program(g, core, T, topo):
+    rank = T.rank_of(core)
+    if rank is None:
+        return
+    eng = {"v": g.vector, "s": g.scalar, "t": g.tensor, "g": g, "y": g.sync}
+    qsem = {"v": "qv", "s": "qs", "t": "qt", "g": "qg"}
+    cnt = {q: 0 for q in eng}
+    know = {q: {} for q in eng}
+    snap, wr, rd, bank = {}, {}, {}, {}
+
+    def waits(q, deps):
+        best = {}
+        for s_, n_ in deps:
+            best[s_] = max(best.get(s_, 0), n_)
+        for s_ in sorted(best, key=lambda z: -best[z]):
+            n_ = best[s_]
+            if know[q].get(s_, 0) >= n_:
+                continue
+            eng[q].wait_ge(T.sem[s_], n_)
+            for k2, v2 in list(snap.get((s_, n_), {}).items()) + [(s_, n_)]:
+                know[q][k2] = max(know[q].get(k2, 0), v2)
+
+    def prep(q, R, Wk, X):
+        deps = [wr[k] for k in list(R) + list(Wk) if k in wr]
+        for k in Wk:
+            deps += list(rd.get(k, {}).items())
+        for k in X:
+            deps += [d for d in bank.get(k, {}).items() if d[0] != qsem.get(q)]
+        waits(q, deps)
+
+    def mark(tok, q, R, Wk, X):
+        d = dict(know[q])
+        d[tok[0]] = tok[1]
+        snap[tok] = d
+        for k in R:
+            rd.setdefault(k, {})[tok[0]] = tok[1]
+        for k in Wk:
+            wr[k] = tok
+            rd[k] = {}
+        for k in X:
+            bank.setdefault(k, {})[tok[0]] = tok[1]
+
+    def E(q, call, R=(), Wk=(), X=()):
+        prep(q, R, Wk, X)
+        cnt[q] += 1
+        call(eng[q]).then_inc(T.sem[qsem[q]], 1)
+        mark((qsem[q], cnt[q]), q, R, Wk, X)
+
+    def DMA(q, out, in_, sem, R=(), Wk=()):
+        prep(q, R, Wk, ())
+        eng[q].dma_start(out, in_).then_inc(T.sem[sem], 16)
+        mark((sem, 16), q, R, Wk, ())
+
+    ps = [T["ps%d" % i] for i in range(8)]
+
+    def c1(i):
+        return T.col[:, i:i + 1]
+
+    def mm(out, l, r, a, b, R, X):
+        E("t", lambda e: e.matmul(out, l, r, a, b), R, (), [X])
+
+    def ts(out, i, s1, s2, o1, o2=None, R=(), Wk=(), X=()):
+        if o2 is None:
+            E("v", lambda e: e.tensor_scalar(out, i, s1, None, o1), R, Wk, X)
+        else:
+            E("v", lambda e: e.tensor_scalar(out, i, s1, s2, o1, o2), R, Wk, X)
+
+    def tt(out, a, b, op, R=(), Wk=(), X=()):
+        E("v", lambda e: e.tensor_tensor(out, a, b, op), R, Wk, X)
+
+    def cp(out, i, R=(), Wk=(), X=()):
+        E("v", lambda e: e.tensor_copy(out, i), R, Wk, X)
+
+    def act(out, i, R=(), Wk=(), X=(), bias=0.0, scale=1.0):
+        E("s", lambda e: e.activation(out, i, F.Identity, bias=bias, scale=scale), R, Wk, X)
+
+    def cts(o, i, s1, s2, o1, o2=None, cols=()):
+        ts(T[o][:], T[i][:], s1, s2, o1, o2, [i] + [("col", c) for c in cols or ()], [o])
+
+    def ctt(o, a, b, op):
+        tt(T[o][:], T[a][:], T[b][:], op, [a, b], [o])
+
+    def colv(i, src, s1, s2, o1, o2=None):
+        ts(c1(i), T[src][:], s1, s2, o1, o2, [src], [("col", i)])
+
+    DMA("y", T.ci[:], T.cb[:], "lci", Wk=["ci"])
+    DMA("s", T.wi[:], T.wt[:], "lwt", Wk=["wi"])
+    for i in range(4):
+        DMA("ys"[i % 2], T.xin[:, 1024 * i:1024 * i + 1024], T.x[:, 1024 * i:1024 * i + 1024], "lx%d" % i, Wk=[("xin", i)])
+    for i in range(2):
+        DMA("ys"[i % 2], T.pin[:, 1024 * i:1024 * i + 1024], T.pk[:, 1024 * i:1024 * i + 1024], "lp%d" % i, Wk=[("pin", i)])
+
+    for buf, pat, base, cm in (("pc", [[0, 1]], 0, 1), ("J", [[1, 128]], 0, 0), ("K8", [[1, 16], [0, 8]], 0, 0),
+                               ("G8", [[0, 16], [1, 8]], 0, 0), ("K16", [[1, 16]], 0, 0),
+                               ("iL0", [[1, 2], [32, 16]], 0, 2), ("mL0", [[16, 32]], MEND, 1)):
+        E("g", lambda e: e.iota(T[buf][:], pat, base, cm), (), [buf])
+    for i in (0, 1):
+        E("v", lambda e: e.memset(ps[3 + i][:, 0:128], -7.5), (), (), [3 + i])
+        E("v", lambda e: e.memset(T["Vt%d" % i][:, 0:16], 0.0), (), [("Vt", i)])
+        E("v", lambda e: e.memset(T["SQ%d" % i][:, 0:8], 0.0), (), [("SQ", i)])
+    cts("ki", "pc", 15, None, A.bitwise_and)
+    cts("gi", "pc", 4, None, A.arith_shift_right)
+    cts("Jk", "J", 15, None, A.bitwise_and)
+    cts("Jg", "J", 4, None, A.arith_shift_right)
+    colv(P_, "pc", 0.0, None, A.add)
+    colv(P1, "pc", 1.0, None, A.add)
+    colv(G_, "gi", 0.0, None, A.add)
+    cts("u1", "Jk", 15.0, -16.0, A.is_equal, A.mult)
+    cts("u2", "Jk", 7.0, 1000.0, A.is_equal, A.mult)
+    colv(DBI, "ki", 7.0, -127.5, A.is_equal, A.mult)
+    cts("ID", "J", c1(P_), None, A.is_equal, None, [P_])
+    ctt("u1", "u1", "u2", A.add)
+    cts("BO", "Jg", c1(G_), None, A.is_equal, None, [G_])
+    cts("si", "ki", 8.0, None, A.add)
+    cts("S8", "K8", 8.0, None, A.add)
+    ctt("u1", "u1", "J", A.add)
+    cts("Js", "J", 8.0, None, A.add)
+    cts("si", "si", 15, None, A.bitwise_and)
+    cts("S8", "S8", 15, None, A.bitwise_and)
+    cts("u2", "u1", 1.0, c1(P_), A.add, A.is_equal, [P_])
+    cts("Js", "Js", 15, None, A.bitwise_and)
+    colv(S_, "si", 0.0, None, A.add)
+    ctt("DM", "ID", "u2", A.subtract)
+    cts("v1", "G8", c1(G_), None, A.is_equal, None, [G_])
+    cts("v2", "S8", c1(S_), None, A.is_le, None, [S_])
+    cts("wb", "wi", 0.0, None, A.add)
+    colv(WF, "wi", 0.0, None, A.add)
+    ctt("EK", "v1", "v2", A.mult)
+    act(T.ID16[:], T.ID[:], ["ID"], ["ID16"])
+    act(T.NID[:], T.ID[:], ["ID"], ["NID"], scale=-1.0)
+    act(T.NID16[:], T.ID[:], ["ID"], ["NID16"], scale=-1.0)
+    act(T.BOf[:], T.BO[:], ["BO"], ["BOf"])
+    cts("BW", "BO", c1(WF), None, A.mult, None, [WF])
+    for o, i in (("LO", "BO"), ("LW", "BW")):
+        for q in range(16):
+            E("g", lambda e: e.affine_select(T[o][:, 128 * q:128 * q + 128], T[i][:], [[0, 8], [1, 16]], A.is_equal, 0.0, -q, 0),
+              [i], [(o, q)])
+    colv(K_, "ki", 0.0, None, A.add)
+    colv(K1, "ki", 1.0, None, A.add)
+    colv(IS15, "ki", 15.0, None, A.is_equal)
+    colv(WSC, "ki", 15.0, None, A.not_equal)
+    cts("u1", "Js", -7.0, 512.0, A.add, A.mult)
+    cts("colk", "K16", c1(K1), -512.0, A.is_equal, A.mult, [K1])
+    cts("u2", "J", c1(P1), None, A.is_equal, None, [P1])
+    cts("u1", "u1", c1(IS15), c1(WSC), A.mult, A.add, [IS15, WSC])
+    cts("colk", "colk", c1(IS15), None, A.add, None, [IS15])
+    ctt("u2", "u2", "BO", A.mult)
+    ctt("BS", "u1", "BO", A.mult)
+    colv(THR, "ki", 0.0, 1.0e6, A.is_equal, A.mult)
+    ctt("DC", "ID", "u2", A.subtract)
+    for k in range(1, 16):
+        ts(T.PL[:, 128 * k:128 * k + 128], T.BS[:], T.colk[:, k:k + 1], None, A.mult, None, ["BS", "colk"], [("PL", k)])
+    ts(c1(THR), c1(THR), 96.25, None, A.add, None, [("col", THR)], [("col", THR)])
+    for h in (0, 1):
+        cp(T.cU_0[:, 256 * h:256 * h + 256], T.ci[:, h::2], ["ci"], [("cU", 0, 2 * h), ("cU", 0, 2 * h + 1)])
+    mm(ps[4][:, 300:301], T.BO[:], T.wb[:], True, True, ["BO", "wb"], 4)
+    colv(G32, "gi", 32.0, None, A.mult)
+    colv(G16, "gi", 16.0, None, A.mult)
+    cts("u1", "K8", c1(K_), None, A.is_equal, None, [K_])
+    cts("u2", "Js", c1(S_), None, A.is_le, None, [S_])
+    cts("iL", "iL0", c1(G32), None, A.subtract, None, [G32])
+    cts("mL", "mL0", c1(G16), None, A.subtract, None, [G16])
+    ctt("DK", "u1", "v1", A.mult)
+    ctt("SX", "u2", "BO", A.mult)
+    ts(c1(H0), ps[4][:, 300:301], 127.5, None, A.mult, None, (), [("col", H0)], [4])
+
+    for i in range(8):
+        sl, X = slice(512 * i, 512 * i + 512), (0, 1, 2, 5, 6, 7)[i % 6]
+        mm(ps[X][:], T.DM[:], T.xin[:, sl], True, True, ["DM", ("xin", i // 2)], X)
+        if i in (3, 7):
+            ts(T.Dt[:, sl], ps[X][:], c1(DBI), None, A.add, None, [("col", DBI)], [("Dt", i)], [X])
+        else:
+            act(T.Dt[:, sl], ps[X][:], [("col", DBI)], [("Dt", i)], [X], bias=c1(DBI))
+    Dk = [("Dt", i) for i in range(8)]
+    Bk = [("Bt", i) for i in range(8)]
+
+    def unpack(i):
+        s, n = i // 2, 1024 * (i // 2) + 512 * (i % 2)
+        j = T.pin[:, n:n + 512]
+        ts(T.Bt[:, n:n + 512], j, 4095, None, A.bitwise_and, None, [("pin", s)], [("Bt", i)])
+        ts(T.Bt[:, 2048 + n:2560 + n], j, 12, None, A.arith_shift_right, None, [("pin", s)], [("Bt", 4 + i)])
+
+    BM, MB = [("Bm", 0), ("Bm", 2)], (5, 5, 0, 0)
+    ones = T.EK[:, 64:72]
+
+    def keys(n, a, m):
+        return [(n, x) for x in range(a // 16, (a + m) // 16)]
+
+    def gath(q, dst, win, t, a, n, R, Wk, bias=0.0):
+        w = win.indirect(T["cU_%d" % t][:, a:a + n])
+        out = dst[:, 16 * a:16 * (a + n)]
+        R = R + [("cU", t, x) for x in range(a // 128, (a + n + 127) // 128)]
+        if q == "s":
+            act(out, w, R, Wk, bias=bias)
+        elif bias:
+            ts(out, w, bias, None, A.add, None, R, Wk)
+        else:
+            cp(out, w, R, Wk)
+
+    def xg(q, t, a, n):
+        gath(q, T.G, T.Dt[:, 0:W], t, a, n, Dk, keys("G", a, n))
+
+    def bg(q, t, a, n):
+        gath(q, T.GB, T.Bt[:, 0:W], t, a, n, Bk, keys("GB", a, n), -2048.0)
+
+    def Gk(b):
+        return keys("G", 128 * b, 128)
+
+    def ediag(b):
+        X = 3 + b % 2
+        for k in range(15):
+            mm(ps[X][:, k:128:16], T.G[:, 2048 * b + k:2048 * b + 2048:16], T.EK[:, 8 * k:8 * k + 8], True, True, Gk(b) + ["EK"], X)
+
+    def zone1(b):
+        X, h, i = 3 + b % 2, 128 * (b % 2), b % 2
+        C = 1.5 * 2.0 ** 27
+        return [lambda: ts(T.R1[:, h:h + 128], ps[X][:, 0:128], C, C, A.add, A.subtract, (), [("R1", i)], [X]),
+                lambda: tt(T.wT[:, h:h + 128], ps[X][:, 0:128], T.R1[:, h:h + 128], A.subtract, [("R1", i)], [("wT", i)], [X])]
+
+    def zone2(b):
+        X, h, i = 3 + b % 2, 128 * (b % 2), b % 2
+        mm(ps[X][:, 128:256], T.wT[:, h:h + 128], T.ID[:], True, True, [("wT", i), "ID"], X)
+
+    def zone3(b):
+        X, h, i = 3 + b % 2, 128 * (b % 2), b % 2
+        ts(T.Wz[:, h:h + 128], ps[X][:, 128:256], c1(WSC), c1(IS15), A.mult, A.add, [("col", WSC), ("col", IS15)], [("Wz", i)], [X])
+
+    CH = ((1, 2, 3, 4), (5, 6, 7, 8), (9, 10, 11, 12), (13, 14, 15))
+
+    def pen(b, c):
+        X, h = (4 * b + c) % 3, 128 * (b % 2)
+        for i, k in enumerate(CH[c]):
+            mm(ps[X][:, 128 * i:128 * i + 128], T.PL[:, 128 * k:128 * k + 128], T.Wz[:, h:h + 128], True, True,
+               [("PL", k), ("Wz", b % 2)], X)
+
+    def sel(b, c, later=False):
+        X, h = (4 * b + c) % 3, 2048 * (b % 2)
+        calls = [lambda i=i, k=k: tt(T.VM[:, h + 128 * k:h + 128 * k + 128], T.G[:, 2048 * b + k:2048 * b + 2048:16],
+                                     ps[X][:, 128 * i:128 * i + 128], A.min, Gk(b), [("VM", b % 2, k)], [X])
+                 for i, k in enumerate(CH[c])]
+        if later:
+            return calls
+        for f in calls:
+            f()
+
+    def sums(b, c):
+        X, h = 5 + b % 2, 2048 * (b % 2)
+        if c == 0:
+            mm(ps[X][:, 0:128:16], T.G[:, 2048 * b:2048 * b + 2048:16], T.EK[:, 0:8], True, True, Gk(b) + ["EK"], X)
+        for k in CH[c]:
+            mm(ps[X][:, k:128:16], T.VM[:, h + 128 * k:h + 128 * k + 128], ones, True, True, [("VM", b % 2, k), "EK"], X)
+
+    def square(b):
+        i = b % 2
+        E("s", lambda e: e.activation(T["SQ%d" % i][:, 1:129], T.wT[:, 128 * i:128 * i + 128], F.Square, bias=120.0, scale=16.0),
+          [("wT", i)], [("SQ", i)])
+
+    def vcopy(b):
+        X = 5 + b % 2
+        tt(T["Vt%d" % (b % 2)][:, 1:129], ps[X][:, 0:128], T["SQ%d" % (b % 2)][:, 0:128], A.add, [("SQ", b % 2)], [("Vt", b % 2)], [X])
+
+    def turn(b):
+        X, V, K = 5 + b % 2, T["Vt%d" % (b % 2)], [("Vt", b % 2)]
+        mm(ps[X][:, 128:256], V[:, 1:129], T.ID[:], True, True, K + ["ID"], X)
+        if b == 3:
+            mm(ps[X][:, 256:384], V[:, 1:129], T.ID[:], True, False, K + ["ID"], X)
+            mm(ps[X][:, 256:384], V[:, 0:128], T.NID[:], False, True, K + ["NID"], X)
+
+    def vs(b):
+        X, j = 5 + b % 2, 128 * b
+        cp(T.VS[:, j:j + 128], ps[X][:, 128:256], (), [("VS", b)], [X])
+
+    def diff(b):
+        X, j = 5 + b % 2, 128 * b
+        mm(ps[X][:, 256:384], T.DC[:], T.VS[:, j:j + 128], True, True, [("VS", b), "DC"], X)
+
+    def cracks(b):
+        X, j = 5 + b % 2, 128 * b
+        return [lambda: ts(T.nd[:], ps[X][:, 256:384], -1.0, None, A.mult, None, (), ["nd"], [X]),
+                lambda: tt(T.ad[:], ps[X][:, 256:384], T.nd[:], A.max, ["nd"], ["ad"], [X]),
+                lambda: ts(T.CC[:, j:j + 128], T.ad[:], c1(THR), None, A.is_gt, None, ["ad", ("col", THR)], [("CC", b)])]
+
+    VSk = [("VS", b) for b in range(4)]
+    CCk = [("CC", b) for b in range(4)]
+    sent = [0]
+
+    def send(t, out, src, R):
+        to = T.cores[(rank + 1 + t % 3) % len(T.cores)]
+        eg = topo.engines(core, to)[:8]
+        rid, pid, _ = topo.addr(to)
+        waits("g", [wr[k] for k in R])
+        g.remote_dma(out, src, T.sem["arr%d" % t], T.sem.loc, pid, rid, sum(1 << x for x in eg))
+        sent[0] += len(eg)
+        return len(eg)
+
+    def g5(t, a, n):
+        cp(T["cU_%d" % t][:, a:a + n], T.Bt[:, 0:DUMP].indirect(T.nx[:, a // 16:(a + n) // 16]), Bk + BM + ["nx"],
+           [("cU", t, x) for x in range(a // 128, (a + n) // 128)])
+
+    for t in range(ROUNDS):
+        cU, c16, Dn, pU = T["cU_%d" % t], T["c16_%d" % t], T["Dn_%d" % t], T["pU_%d" % t]
+        C16 = [("c16", t)]
+        last = t == ROUNDS - 1
+
+        def bdiag(b, k0=1, k1=16):
+            X = (2, 6)[b % 2]
+            for k in range(k0, k1):
+                mm(ps[X][:, k:128:16], T.GB[:, 2048 * b + k:2048 * b + 2048:16], T.DK[:, 8 * k:8 * k + 8], True, True,
+                   keys("GB", 128 * b, 128) + ["DK"], X)
+
+        xg("s", t, 64, 64)
+        xg("v", t, 0, 64)
+        xg("v", t, 128, 32)
+        xg("s", t, 160, 96)
+        ediag(0)
+        Z = zone1(0)
+        Z[0]()
+        if t:
+            g5(t, 256, 256)
+        Z[1]()
+        send(t, T["rC_%d" % t][:], cU[:, 256:512], [("cU", t, x) for x in range(4)])
+        zone2(0)
+        zone3(0)
+        square(0)
+        xg("s", t, 256, 128)
+        ts(c16[:], cU[:], -2048.0, None, A.add, None, [("cU", t, x) for x in range(4)], C16)
+        for b in range(NB):
+            C, Z, nop = [], [], (lambda: 0)
+            pen(b, 0)
+            pen(b, 1)
+            if b:
+                turn(b - 1)
+                C = cracks(b - 1)
+            sel(b, 0)
+            if b:
+                vs(b - 1)
+                diff(b - 1)
+            sel(b, 1)
+            if t == 0 and b < 2:
+                unpack(2 * b)
+            pen(b, 2)
+            if b < 3:
+                ediag(b + 1)
+            pen(b, 3)
+            if b < 3:
+                Z = zone1(b + 1)
+                fg, a = (xg, 384) if b == 0 else (bg, 128 * b - 128 if t else 0)
+            C, Z = C or [nop] * 3, Z or [nop] * 2
+            sums(b, 0)
+            S = sel(b, 2, True) + sel(b, 3, True)
+            for f in (C[0], S[0], C[1], S[1], C[2], S[2], Z[0], S[3], Z[1], S[4]):
+                f()
+            if b < 3:
+                if t or b != 1:
+                    fg("s", t, a, 64)
+                square(b + 1)
+                if t or b != 1:
+                    fg("s", t, a + 64, 64)
+                zone2(b + 1)
+            sums(b, 1)
+            for f in S[5:]:
+                f()
+            if b < 3:
+                zone3(b + 1)
+            if t == 0 and b < 2:
+                unpack(2 * b + 1)
+            sums(b, 2)
+            sums(b, 3)
+            vcopy(b)
+        for b in (2,) if t else (1, 2):
+            bg("s", t, 128 * b, 128)
+        bg("s", t, 384, 64)
+        mm(ps[1][:, 0:256], T.DM[:], T.VS[:, 0:256], True, True, VSk[:2] + ["DM"], 1)
+        turn(3)
+        bdiag(0, 1, 6)
+        vs(3)
+        C = cracks(3)
+        C[0]()
+        cp(Dn[:, 0:256], ps[1][:, 0:256], (), [("Dn", t, 0)], [1])
+        C[1]()
+        mm(ps[0][:, 0:256], T.DM[:], T.VS[:, 256:512], True, True, VSk[2:] + ["DM"], 0)
+        cp(Dn[:, 256:512], ps[0][:, 0:256], (), [("Dn", t, 1)], [0])
+        C[2]()
+        for q in range(16):
+            mm(ps[3][:, 256:288], T.LW[:, 128 * q:128 * q + 128], T.VS[:, q::16], q == 0, q == 15, VSk + [("LW", q)], 3)
+        for q in range(16):
+            mm(ps[4][:, 256:288], T.LO[:, 128 * q:128 * q + 128], T.CC[:, q::16], q == 0, q == 15, CCk + [("LO", q)], 4)
+        bg("v", t, 480, 32)
+        ts(T.Hs[:], ps[3][:, 256:288], c1(H0), None, A.add, None, [("col", H0)], ["Hs"], [3])
+        E("v", lambda e: e.tensor_reduce(T.Rr[:], ps[4][:, 256:288], AxisListType.X, A.add), (), ["Rr"], [4])
+        mm(ps[3][:, 320:321], T.BOf[:], T.Rr[:], True, True, ["BOf", "Rr"], 3)
+        send(t, T["rD_%d" % t][:], Dn[:, 256:512], [("Dn", t, 1)])
+        ts(T.na[:], ps[4][:, 256:288], 5.5, float(DUMP), A.is_gt, A.mult, (), ["na"], [4])
+        ts(T.na1[:], ps[4][:, 256:288], 5.5, None, A.is_gt, None, (), ["na1"], [4])
+        ctt("rp", "na", "iL", A.add)
+        ctt("y1", "na1", "mL", A.mult)
+        Ac = ps[3][:, 320:321]
+        ts(T.i1[:], T.Hs[:], Ac, 512.0, A.add, A.mult, ["Hs"], ["i1"], [3])
+        ts(T.x1[:], T.Hs[:], 37.0, Ac, A.mult, A.add, ["Hs"], ["x1"], [3])
+        cts("i2", "i1", 3584, None, A.bitwise_and)
+        cts("x2", "x1", 4095, None, A.bitwise_and)
+        ctt("pf", "i2", "rp", A.add)
+        ctt("y3", "x2", "y1", A.max)
+        cp(pU[:], T.pf[:], ["pf"], [("pU", t)])
+        cp(T.nx[:], T.y3[:], ["y3"], ["nx"])
+        ne = 3 * send(t, T["rP_%d" % t][:], pU[:, 16:32], [("pU", t)])
+
+        def bturn(b):
+            s = slice(128 * b, 128 * b + 128)
+            act(T.BT[:, s], ps[(2, 6)[b % 2]][:, 0:128], (), [("BT", b)], [(2, 6)[b % 2]])
+            X = MB[b]
+            mm(ps[X][:, s], T.BT[:, s], T.ID16[:], True, False, [("BT", b), "ID16"], X)
+            mm(ps[X][:, s], T.NID16[:], c16[:, s], False, True, C16 + ["NID16"], X)
+
+        def mend(a, z):
+            s = slice(128 * a, 128 * z)
+            tt(T.t2[:, s], ps[MB[a]][:, s], T.CC[:, s], A.mult, [("CC", b) for b in range(a, z)], [("t2", a)], [MB[a]])
+            tt(T.Bt[:, MEND + 128 * a:MEND + 128 * z], T.t2[:, s], ps[7][:, s], A.add, [("t2", a)], [("Bm", a)], [7])
+
+        cp(T.Dt[:].indirect(pU[:, 0:16]), Dn[:, 0:256], [("pU", t), ("Dn", t, 0)], Dk)
+        bg("v", t, 448, 32)
+        bdiag(0, 6, 16)
+        for b in range(NB):
+            if b < 3:
+                bdiag(b + 1)
+            bturn(b)
+            if b in (0, 1):
+                act(ps[7][:, 256 * b:256 * b + 256], c16[:, 256 * b:256 * b + 256], C16, (), [7], bias=2048.0)
+        cp(T.Bt[:].indirect(pU[:, 0:16]), cU[:, 0:256], [("pU", t), ("cU", t, 0), ("cU", t, 1)], Bk + BM)
+        mend(0, 2)
+        wr[("arr", t)] = ("arr%d" % t, ne)
+        rP = T["rP_%d" % t][:]
+        win = T.Bt[:, 0:DUMP]
+        B5 = Bk + BM + ["nx"]
+
+        def rscat(w):
+            if w:
+                cp(T.Dt[:].indirect(rP), T["rD_%d" % t][:], [("arr", t)], Dk)
+            else:
+                cp(T.Bt[:].indirect(rP), T["rC_%d" % t][:], [("arr", t)], Bk + BM)
+
+        rscat(last)
+        if last:
+            rscat(False)
+        mend(2, 4)
+        if not last:
+            rscat(True)
+            g5(t + 1, 0, 128)
+            g5(t + 1, 128, 128)
+        else:
+            for h in (0, 1):
+                cp(T.ycs[:, h::2], win.indirect(T.nx[:, 16 * h:16 * h + 16]), B5, [("yc", h)])
+
+    for i in range(8):
+        sl = slice(512 * i, 512 * i + 512)
+        X = (1, 2, 3, 4, 6, 1, 2, 3)[i]
+        mm(ps[X][:], T.SX[:], T.Dt[:, sl], True, True, Dk + ["SX"], X)
+        if i < 6:
+            E("s", lambda e: e.activation(T.xin[:, sl], ps[X][:], F.Copy, bias=127.5), (), [("xo", i)], [X])
+        else:
+            ts(T.xin[:, sl], ps[X][:], 127.5, None, A.add, None, (), [("xo", i)], [X])
+        if i % 2:
+            c = slice(512 * (i - 1), 512 * (i + 1))
+            DMA("y", T.yx[:, c], T.xin[:, c], "o%d" % (i // 2), [("xo", i - 1), ("xo", i)])
+    DMA("s", T.yc[:], T.ycs[:], "o4", [("yc", 0), ("yc", 1)])
+    waits("g", [(s_, 16) for s_ in SEMAPHORES if s_[0] == "o" or (s_[0] == "l" and s_ != "loc")])
+    waits("g", [("loc", sent[0])] + [(qsem[q], cnt[q]) for q in qsem])

@@ -7,24 +7,29 @@ NB = 4
 W = 4096
 MEND = 4096
 DUMP = 4608
-WIN = DUMP + 4096
 LONG = {"f": "float32", "b": "bfloat16", "h": "float16", "i": "int32", "u": "uint16"}
 SCRATCH = {}
-_spec = """Dt:8704b Bt:8704i xin:4096b pin:2048i ci:512i wi:1i G:8192b GB:8192h VM:4096b R1:256f wT:256b Wz:256b SQ0:136f SQ1:136f
-Vt0:144b Vt1:144b VS:512b CC:512b nd:128b ad:128b BT:512h t2:512f ycs:512f Rr:1f Hs:32f na:32f na1:32f rp:32f
-i1:32i i2:32i pf:32f x1:32i x2:32i y1:32f y3:32f nx:32u pc:1i ki:1i gi:1i si:1i col:32f wb:1b J:128i Jk:128i Js:128i
-Jg:128i K8:128i S8:128i G8:128i K16:16i iL:32f mL:32f iL0:32i mL0:32i u1:128f u2:128f v1:128f v2:128f colk:16f
-BO:128b BW:128b BOf:128f BS:128b ID:128b NID:128b ID16:128h NID16:128h EK:128b DK:128h DM:128b DC:128b SX:128b
+_spec = """Xt:8704b Bt:8704i pin:2048i ci:512i wi:1i G:8192b GB:8192h VM:4096b R1:256b U:256b Wn:512b Vt:256b
+CC:512b BT:512h cF:512f ycs:512f Ac:1f Hs:32f na:32f na1:32f rp:32f
+i1:32i i2:32i pf:32f x1:32i x2:32i y1:32f y3:32f nx:32u pc:1i ki:1i gi:1i col:32f J:128i Jk:128i Jg:128i JK:128i G8:8i
+I2:2i G2:2i K2:2i GF:2f KF:2f TG:2f K8:16i iL:32f mL:32f iL0:32i mL0:32i u1:128f u2:128f colm:16f TP:128f mA:128f mB:128f
+BO:128b BW:128b ID:128b ID16:128h NID16:128h DKz:136b DK:128h DC:128b E0:128b ON:8b CFA:128b CFB:128b CQA:128b CQB:128b
 PL:2048b LO:2048b LW:2048b"""
 for _t in range(ROUNDS):
-    _spec += " cU_%d:512u c16_%d:512h Dn_%d:512b pU_%d:32u rC_%d:256u rD_%d:256b rP_%d:16u" % ((_t,) * 7)
+    _spec += " cU_%d:512u c16_%d:512h VS_%d:512b pU_%d:32u rC_%d:256u rD_%d:256b rP_%d:16u" % ((_t,) * 7)
 for _w in _spec.split():
     _n, _d = _w.split(":")
     SCRATCH[_n] = ("sbuf", [128, int(_d[:-1])], LONG[_d[-1]])
 for _t in range(8):
     SCRATCH["ps%d" % _t] = ("psum", [128, 512], "float32")
-SEMAPHORES = "qv qs qt qg loc lci lwt lx0 lx1 lx2 lx3 lp0 lp1 arr0 arr1 arr2 arr3 o0 o1 o2 o3 o4".split()
-K_, G_, S_, P_, P1, G16, G32, IS15, WSC, THR, DBI, H0, WF, K1 = range(14)
+SEMAPHORES = "qv qs qt qg loc lci lwt lx0 lx1 lp0 lp1 arr0 arr1 arr2 arr3 o0 o1 o2 o3 o4".split()
+K_, G_, P_, P1, G16, G32, WF, B8, Q38, I0, NI0, K0, HM = range(13)
+VB, VP = 80, 8
+SHARE_V = ((("x", 0, 64), ("x", 128, 160)), (("x", 160, 192),), (), ()), \
+          ((("x", 0, 64), ("x", 128, 160)), (("x", 160, 176),), (("x", 368, 384),), (("x", 496, 512),))
+SHARE_S = ((("x", 64, 128), ("x", 192, 256)), (("x", 256, 352),), (("x", 352, 384), ("x", 384, 512)), (("b", 0, 64),), (("b", 64, 256), ("b", 256, 288))), \
+          ((("x", 64, 128), ("x", 176, 256)), (("x", 256, 352),), (("x", 352, 368), ("x", 384, 448)), (("x", 448, 496), ("b", 0, 48)), (("b", 48, 256), ("b", 256, 288)))
+UP = ((0, 1, 2, 3), (), (), ())
 
 
 def rank_program(g, core, T, topo):
@@ -100,11 +105,14 @@ def rank_program(g, core, T, topo):
     def cp(out, i, R=(), Wk=(), X=()):
         E("v", lambda e: e.tensor_copy(out, i), R, Wk, X)
 
-    def act(out, i, R=(), Wk=(), X=(), bias=0.0, scale=1.0):
-        E("s", lambda e: e.activation(out, i, F.Identity, bias=bias, scale=scale), R, Wk, X)
+    def act(out, i, R=(), Wk=(), X=(), bias=0.0, scale=1.0, fn=F.Identity):
+        E("s", lambda e: e.activation(out, i, fn, bias=bias, scale=scale), R, Wk, X)
+
+    def fill(ap, c, Wk):
+        E("v", lambda e: e.memset(ap, c), (), Wk)
 
     def cts(o, i, s1, s2, o1, o2=None, cols=()):
-        ts(T[o][:], T[i][:], s1, s2, o1, o2, [i] + [("col", c) for c in cols or ()], [o])
+        ts(T[o][:], T[i][:], s1, s2, o1, o2, [i] + [("col", c) if isinstance(c, int) else c for c in cols or ()], [o])
 
     def ctt(o, a, b, op):
         tt(T[o][:], T[a][:], T[b][:], op, [a, b], [o])
@@ -112,96 +120,96 @@ def rank_program(g, core, T, topo):
     def colv(i, src, s1, s2, o1, o2=None):
         ts(c1(i), T[src][:], s1, s2, o1, o2, [src], [("col", i)])
 
+    def iota(out, pat, base, cm, key, **kw):
+        E("g", lambda e: e.iota(out, pat, base, cm, **kw), (), [key])
+
+    Xk, Bk = ["X0", "X1"], [("Bt", i) for i in range(8)]
     DMA("y", T.ci[:], T.cb[:], "lci", Wk=["ci"])
     DMA("s", T.wi[:], T.wt[:], "lwt", Wk=["wi"])
-    for i in range(4):
-        DMA("ys"[i % 2], T.xin[:, 1024 * i:1024 * i + 1024], T.x[:, 1024 * i:1024 * i + 1024], "lx%d" % i, Wk=[("xin", i)])
     for i in range(2):
-        DMA("ys"[i % 2], T.pin[:, 1024 * i:1024 * i + 1024], T.pk[:, 1024 * i:1024 * i + 1024], "lp%d" % i, Wk=[("pin", i)])
+        DMA("ys"[i], T.Xt[:, 2048 * i:2048 * i + 2048], T.x[:, 2048 * i:2048 * i + 2048], "lx%d" % i, Wk=[Xk[i]])
+    for i in range(2):
+        DMA("ys"[i], T.pin[:, 1024 * i:1024 * i + 1024], T.pk[:, 1024 * i:1024 * i + 1024], "lp%d" % i, Wk=[("pin", i)])
 
-    for buf, pat, base, cm in (("pc", [[0, 1]], 0, 1), ("J", [[1, 128]], 0, 0), ("K8", [[1, 16], [0, 8]], 0, 0),
-                               ("G8", [[0, 16], [1, 8]], 0, 0), ("K16", [[1, 16]], 0, 0),
-                               ("iL0", [[1, 2], [32, 16]], 0, 2), ("mL0", [[16, 32]], MEND, 1)):
-        E("g", lambda e: e.iota(T[buf][:], pat, base, cm), (), [buf])
-    for i in (0, 1):
-        E("v", lambda e: e.memset(ps[3 + i][:, 0:128], -7.5), (), (), [3 + i])
-        E("v", lambda e: e.memset(T["Vt%d" % i][:, 0:16], 0.0), (), [("Vt", i)])
-        E("v", lambda e: e.memset(T["SQ%d" % i][:, 0:8], 0.0), (), [("SQ", i)])
+    iota(T.pc[:], [[0, 1]], 0, 1, "pc")
+    iota(T.I2[:], [[55, 2]], 7, 1, "I2")
+    iota(T.Jg[:], [[1, 8], [0, 16]], 0, 0, "Jg")
+    for buf, pat, base, cm in (("J", [[1, 128]], 0, 0), ("Jk", [[0, 8], [1, 16]], 0, 0), ("JK", [[1, 16], [16, 8]], 0, 0),
+                               ("K8", [[7, 2], [1, 8]], 0, 0)):
+        iota(T[buf][:], pat, base, cm, buf)
+    iota(T.TP[:], [[0, 8], [-256, 2], [32, 8]], 0, 0, ("TP", 0), allow_small_or_imprecise_dtypes=True)
+    wr[("TP", 1)] = wr[("TP", 0)]
+    for buf, pat, base, cm in (("G8", [[1, 8]], 0, 0), ("iL0", [[1, 2], [32, 16]], 0, 2), ("mL0", [[16, 32]], MEND, 1)):
+        iota(T[buf][:], pat, base, cm, buf)
+    fill(T.U[:], 0.0, [("U", 0), ("U", 1)])
+    fill(T.DKz[:], 0.0, ["DKz"])
     cts("ki", "pc", 15, None, A.bitwise_and)
     cts("gi", "pc", 4, None, A.arith_shift_right)
-    cts("Jk", "J", 15, None, A.bitwise_and)
-    cts("Jg", "J", 4, None, A.arith_shift_right)
     colv(P_, "pc", 0.0, None, A.add)
+    colv(I0, "pc", 0.0, None, A.is_equal)
+    colv(NI0, "pc", 0.0, None, A.not_equal)
+    colv(B8, "pc", 64.0, 8.0, A.is_lt, A.mult)
+    colv(Q38, "pc", 64.0, 3808.0, A.is_ge, A.mult)
     colv(P1, "pc", 1.0, None, A.add)
     colv(G_, "gi", 0.0, None, A.add)
-    cts("u1", "Jk", 15.0, -16.0, A.is_equal, A.mult)
-    cts("u2", "Jk", 7.0, 1000.0, A.is_equal, A.mult)
-    colv(DBI, "ki", 7.0, -127.5, A.is_equal, A.mult)
-    cts("ID", "J", c1(P_), None, A.is_equal, None, [P_])
-    ctt("u1", "u1", "u2", A.add)
+    colv(K0, "ki", 0.0, None, A.is_equal)
+    cts("G2", "I2", 7, None, A.bitwise_and)
+    cts("K2", "I2", 3, None, A.arith_shift_right)
+    colv(HM, "pc", 64.0, -8.0, A.is_ge, A.mult)
+    colv(G16, "gi", 16.0, None, A.mult)
+    cts("GF", "G2", 0.0, None, A.add)
+    ts(T.KF[:, 0:1], T.K2[:, 0:1], c1(HM), -1.0, A.add, A.add, ["K2", ("col", HM)], [("KF", 0)])
+    ts(T.KF[:, 1:2], T.K2[:, 1:2], c1(HM), c1(NI0), A.add, A.mult, ["K2", ("col", HM), ("col", NI0)], [("KF", 1)])
+    cts("TG", "G2", 16.0, 1.0, A.mult, A.add)
     cts("BO", "Jg", c1(G_), None, A.is_equal, None, [G_])
-    cts("si", "ki", 8.0, None, A.add)
-    cts("S8", "K8", 8.0, None, A.add)
-    ctt("u1", "u1", "J", A.add)
-    cts("Js", "J", 8.0, None, A.add)
-    cts("si", "si", 15, None, A.bitwise_and)
-    cts("S8", "S8", 15, None, A.bitwise_and)
-    cts("u2", "u1", 1.0, c1(P_), A.add, A.is_equal, [P_])
-    cts("Js", "Js", 15, None, A.bitwise_and)
-    colv(S_, "si", 0.0, None, A.add)
-    ctt("DM", "ID", "u2", A.subtract)
-    cts("v1", "G8", c1(G_), None, A.is_equal, None, [G_])
-    cts("v2", "S8", c1(S_), None, A.is_le, None, [S_])
-    cts("wb", "wi", 0.0, None, A.add)
+    cts("mA", "Jg", T.GF[:, 0:1], c1(I0), A.is_equal, A.max, ["GF", I0])
+    tt(T.TG[:], T.TG[:], T.KF[:], A.add, ["TG", ("KF", 0), ("KF", 1)], ["TG"])
+    cts("mB", "Jg", T.GF[:, 1:2], c1(I0), A.is_equal, A.max, ["GF", I0])
+    cts("ID", "J", c1(P_), None, A.is_equal, None, [P_])
+    cts("u1", "J", c1(P1), None, A.is_equal, None, [P1])
+    cts("u2", "Jk", 0.5, 85.0 / 64, A.is_gt, A.mult)
+    ctt("u1", "ID", "u1", A.subtract)
+    colv(G32, "gi", 32.0, None, A.mult)
+    cts("ID16", "ID", 1.0, None, A.mult)
+    ctt("DC", "u1", "u2", A.mult)
+    cts("NID16", "ID", -1.0, None, A.mult)
+    cts("DK", "JK", c1(P_), None, A.is_equal, None, [P_])
+    for h in (0, 1):
+        cp(T.cU_0[:, 256 * h:256 * h + 256], T.ci[:, h::2], ["ci"], [("cU", 0, 2 * h), ("cU", 0, 2 * h + 1)])
+    act(T.TP[0:1, :], T.TP[0:1, :], [("TP", 0)], [("TP", 0)], bias=8.0, scale=1.0 / 16, fn=F.Square)
+    ts(T.TP[64:128, :], T.TP[64:128, :], -1.0, -256.0, A.mult, A.add, [("TP", 1)], [("TP", 1)])
+    ts(T.TP[0:1, :], T.TP[0:1, :], -1.0, 68.0, A.mult, A.add, [("TP", 0)], [("TP", 0)])
+    fill(T.TP[64:128, 8::16], 32.0, [("TP", 1)])
+    ts(T.colm[:, 0:8], T.K8[:, 0:8], T.KF[:, 0:1], c1(I0), A.is_equal, A.max, ["K8", ("KF", 0), ("col", I0)], [("cm", 0)])
+    fill(T.TP[0:64, 8::16], 0.0, [("TP", 0)])
+    ts(T.colm[:, 8:9], T.K8[:, 8:9], T.KF[:, 1:2], None, A.is_equal, None, ["K8", ("KF", 1)], [("cm", 1)])
+    fill(T.TP[0:1, 8::16], -28.0, [("TP", 0)])
+    ts(T.colm[:, 9:16], T.K8[:, 9:16], T.KF[:, 1:2], c1(I0), A.is_equal, A.max, ["K8", ("KF", 1), ("col", I0)], [("cm", 2)])
+    ts(T.DKz[:, 1:64], T.JK[:, 0:63], c1(P_), None, A.is_equal, None, ["JK", ("col", P_)], ["DKz"])
+    for o, m in (("CFA", "mA"), ("CFB", "mB")):
+        tt(T[o][:], T.TP[:], T[m][:], A.mult, [("TP", 0), ("TP", 1), m], [o])
+    ts(T.DKz[:, 65:130], T.JK[:, 63:128], c1(P_), None, A.is_equal, None, ["JK", ("col", P_)], ["DKz"])
+    CM = [("cm", i) for i in range(3)]
+    for j in range(16):
+        o, i, m = T.PL[:, 128 * j:128 * j + 128], ("CFA", "CFB")[j // 8], T.colm[:, j:j + 1]
+        if j % 2:
+            act(o, T[i][:], [i] + CM, [("PL", j)], scale=m)
+        else:
+            ts(o, T[i][:], m, None, A.mult, None, [i] + CM, [("PL", j)])
     colv(WF, "wi", 0.0, None, A.add)
-    ctt("EK", "v1", "v2", A.mult)
-    act(T.ID16[:], T.ID[:], ["ID"], ["ID16"])
-    act(T.NID[:], T.ID[:], ["ID"], ["NID"], scale=-1.0)
-    act(T.NID16[:], T.ID[:], ["ID"], ["NID16"], scale=-1.0)
-    act(T.BOf[:], T.BO[:], ["BO"], ["BOf"])
+    cts("ON", "G8", c1(G_), None, A.is_equal, None, [G_])
+    for o, j, c in (("CQA", 0, 1088.0), ("CQB", 1, 4.0)):
+        cts(o, "J", T.TG[:, j:j + 1], c1(Q38), A.is_equal, A.mult, ["TG", Q38])
     cts("BW", "BO", c1(WF), None, A.mult, None, [WF])
+    for o, j, c in (("CQA", 0, 1088.0), ("CQB", 1, 4.0)):
+        ts(T[o][0:1, :], T.Jk[0:1, :], 0.5, c, A.is_gt, A.mult, ["Jk"], [o])
     for o, i in (("LO", "BO"), ("LW", "BW")):
         for q in range(16):
             E("g", lambda e: e.affine_select(T[o][:, 128 * q:128 * q + 128], T[i][:], [[0, 8], [1, 16]], A.is_equal, 0.0, -q, 0),
               [i], [(o, q)])
-    colv(K_, "ki", 0.0, None, A.add)
-    colv(K1, "ki", 1.0, None, A.add)
-    colv(IS15, "ki", 15.0, None, A.is_equal)
-    colv(WSC, "ki", 15.0, None, A.not_equal)
-    cts("u1", "Js", -7.0, 512.0, A.add, A.mult)
-    cts("colk", "K16", c1(K1), -512.0, A.is_equal, A.mult, [K1])
-    cts("u2", "J", c1(P1), None, A.is_equal, None, [P1])
-    cts("u1", "u1", c1(IS15), c1(WSC), A.mult, A.add, [IS15, WSC])
-    cts("colk", "colk", c1(IS15), None, A.add, None, [IS15])
-    ctt("u2", "u2", "BO", A.mult)
-    ctt("BS", "u1", "BO", A.mult)
-    colv(THR, "ki", 0.0, 1.0e6, A.is_equal, A.mult)
-    ctt("DC", "ID", "u2", A.subtract)
-    for k in range(1, 16):
-        ts(T.PL[:, 128 * k:128 * k + 128], T.BS[:], T.colk[:, k:k + 1], None, A.mult, None, ["BS", "colk"], [("PL", k)])
-    ts(c1(THR), c1(THR), 96.25, None, A.add, None, [("col", THR)], [("col", THR)])
-    for h in (0, 1):
-        cp(T.cU_0[:, 256 * h:256 * h + 256], T.ci[:, h::2], ["ci"], [("cU", 0, 2 * h), ("cU", 0, 2 * h + 1)])
-    mm(ps[4][:, 300:301], T.BO[:], T.wb[:], True, True, ["BO", "wb"], 4)
-    colv(G32, "gi", 32.0, None, A.mult)
-    colv(G16, "gi", 16.0, None, A.mult)
-    cts("u1", "K8", c1(K_), None, A.is_equal, None, [K_])
-    cts("u2", "Js", c1(S_), None, A.is_le, None, [S_])
     cts("iL", "iL0", c1(G32), None, A.subtract, None, [G32])
     cts("mL", "mL0", c1(G16), None, A.subtract, None, [G16])
-    ctt("DK", "u1", "v1", A.mult)
-    ctt("SX", "u2", "BO", A.mult)
-    ts(c1(H0), ps[4][:, 300:301], 127.5, None, A.mult, None, (), [("col", H0)], [4])
-
-    for i in range(8):
-        sl, X = slice(512 * i, 512 * i + 512), (0, 1, 2, 5, 6, 7)[i % 6]
-        mm(ps[X][:], T.DM[:], T.xin[:, sl], True, True, ["DM", ("xin", i // 2)], X)
-        if i in (3, 7):
-            ts(T.Dt[:, sl], ps[X][:], c1(DBI), None, A.add, None, [("col", DBI)], [("Dt", i)], [X])
-        else:
-            act(T.Dt[:, sl], ps[X][:], [("col", DBI)], [("Dt", i)], [X], bias=c1(DBI))
-    Dk = [("Dt", i) for i in range(8)]
-    Bk = [("Bt", i) for i in range(8)]
+    ts(T.E0[:], T.LO[:, 0:128], c1(K0), None, A.mult, None, [("LO", 0), ("col", K0)], ["E0"])
 
     def unpack(i):
         s, n = i // 2, 1024 * (i // 2) + 512 * (i % 2)
@@ -210,12 +218,13 @@ def rank_program(g, core, T, topo):
         ts(T.Bt[:, 2048 + n:2560 + n], j, 12, None, A.arith_shift_right, None, [("pin", s)], [("Bt", 4 + i)])
 
     BM, MB = [("Bm", 0), ("Bm", 2)], (5, 5, 0, 0)
-    ones = T.EK[:, 64:72]
 
     def keys(n, a, m):
-        return [(n, x) for x in range(a // 16, (a + m) // 16)]
+        return [(n, x) for x in range(a // 8, (a + m) // 8)]
 
     def gath(q, dst, win, t, a, n, R, Wk, bias=0.0):
+        if not n:
+            return
         w = win.indirect(T["cU_%d" % t][:, a:a + n])
         out = dst[:, 16 * a:16 * (a + n)]
         R = R + [("cU", t, x) for x in range(a // 128, (a + n + 127) // 128)]
@@ -226,11 +235,11 @@ def rank_program(g, core, T, topo):
         else:
             cp(out, w, R, Wk)
 
-    def xg(q, t, a, n):
-        gath(q, T.G, T.Dt[:, 0:W], t, a, n, Dk, keys("G", a, n))
+    def xg(q, t, a, z):
+        gath(q, T.G, T.Xt[:, 0:W], t, a, z - a, Xk, keys("G", a, z - a))
 
-    def bg(q, t, a, n):
-        gath(q, T.GB, T.Bt[:, 0:W], t, a, n, Bk, keys("GB", a, n), -2048.0)
+    def bg(q, t, a, z):
+        gath(q, T.GB, T.Bt[:, 0:W], t, a, z - a, Bk, keys("GB", a, z - a), -2048.0)
 
     def Gk(b):
         return keys("G", 128 * b, 128)
@@ -238,78 +247,90 @@ def rank_program(g, core, T, topo):
     def ediag(b):
         X = 3 + b % 2
         for k in range(15):
-            mm(ps[X][:, k:128:16], T.G[:, 2048 * b + k:2048 * b + 2048:16], T.EK[:, 8 * k:8 * k + 8], True, True, Gk(b) + ["EK"], X)
+            a, z = (0, 9) if k == 0 else (1 + 8 * k + (k > 7), 9 + 8 * k + (k >= 7))
+            mm(ps[X][:, a:z], T.G[:, 2048 * b + k:2048 * b + 2048:16], T.DKz[:, a:z], True, True, Gk(b) + ["DKz"], X)
 
-    def zone1(b):
+    def near(b):
         X, h, i = 3 + b % 2, 128 * (b % 2), b % 2
         C = 1.5 * 2.0 ** 27
-        return [lambda: ts(T.R1[:, h:h + 128], ps[X][:, 0:128], C, C, A.add, A.subtract, (), [("R1", i)], [X]),
-                lambda: tt(T.wT[:, h:h + 128], ps[X][:, 0:128], T.R1[:, h:h + 128], A.subtract, [("R1", i)], [("wT", i)], [X])]
+        return [lambda: ts(T.R1[:, h:h + 122], ps[X][:, 0:122], C, C, A.add, A.subtract, (), [("R1", i)], [X]),
+                lambda: tt(T.U[:, h:h + 122], ps[X][:, 0:122], T.R1[:, h:h + 122], A.subtract, [("R1", i)], [("U", i)], [X])]
 
-    def zone2(b):
+    def tiles(b):
         X, h, i = 3 + b % 2, 128 * (b % 2), b % 2
-        mm(ps[X][:, 128:256], T.wT[:, h:h + 128], T.ID[:], True, True, [("wT", i), "ID"], X)
+        for j in (0, 1):
+            for p in (0, 64):
+                mm(ps[X][p:p + 64, 128 + 128 * j:256 + 128 * j], T.U[:, h + 64 * j:h + 64 * j + 64], T.ID[:], True, True,
+                   [("U", i), "ID"], X)
+        act(T.Wn[:, 2 * h:2 * h + 256], ps[X][:, 128:384], [("col", B8)], [("Wn", i)], [X], bias=c1(B8), fn=F.Square)
 
-    def zone3(b):
-        X, h, i = 3 + b % 2, 128 * (b % 2), b % 2
-        ts(T.Wz[:, h:h + 128], ps[X][:, 128:256], c1(WSC), c1(IS15), A.mult, A.add, [("col", WSC), ("col", IS15)], [("Wz", i)], [X])
+    def tile(b, j):
+        a = 256 * (b % 2) + 128 * j
+        return T.Wn[:, a:a + 128]
 
-    CH = ((1, 2, 3, 4), (5, 6, 7, 8), (9, 10, 11, 12), (13, 14, 15))
+    CH = ((1, 5, 9, 13), (2, 6, 10, 14), (3, 7, 11, 15), (4, 8, 12))
 
     def pen(b, c):
-        X, h = (4 * b + c) % 3, 128 * (b % 2)
+        X = (4 * b + c) % 3
         for i, k in enumerate(CH[c]):
-            mm(ps[X][:, 128 * i:128 * i + 128], T.PL[:, 128 * k:128 * k + 128], T.Wz[:, h:h + 128], True, True,
-               [("PL", k), ("Wz", b % 2)], X)
+            js = [k - 1] if k < 8 else [7, 8] if k == 8 else [k]
+            for j in js:
+                mm(ps[X][:, i:512:4], T.PL[:, 128 * j:128 * j + 128], tile(b, j // 8), j == js[0], j == js[-1],
+                   [("PL", j), ("Wn", b % 2)], X)
 
-    def sel(b, c, later=False):
-        X, h = (4 * b + c) % 3, 2048 * (b % 2)
-        calls = [lambda i=i, k=k: tt(T.VM[:, h + 128 * k:h + 128 * k + 128], T.G[:, 2048 * b + k:2048 * b + 2048:16],
-                                     ps[X][:, 128 * i:128 * i + 128], A.min, Gk(b), [("VM", b % 2, k)], [X])
-                 for i, k in enumerate(CH[c])]
-        if later:
-            return calls
-        for f in calls:
-            f()
+    def vm(b, c, i):
+        o = 2048 * (b % 2) + 512 * c
+        return T.VM[:, o + i:o + 512:4]
+
+    def sel(b, c):
+        X, o = (4 * b + c) % 3, 2048 * (b % 2) + 512 * c
+        if c < 3:
+            return [lambda: tt(T.VM[:, o:o + 512], T.G[:, 2048 * b + c + 1:2048 * b + 2048:4], ps[X][:], A.min, Gk(b),
+                               [("VM", b % 2, k) for k in CH[c]], [X])]
+        return [lambda i=i, k=k: tt(vm(b, c, i), T.G[:, 2048 * b + k:2048 * b + 2048:16], ps[X][:, i:512:4], A.min, Gk(b),
+                                    [("VM", b % 2, k)], [X]) for i, k in enumerate(CH[c])]
 
     def sums(b, c):
-        X, h = 5 + b % 2, 2048 * (b % 2)
+        X, g0, Wk = 5 + b % 2, T.G[:, 2048 * b:2048 * b + 2048:16], [("Wn", b % 2), "CQA", "CQB"]
         if c == 0:
-            mm(ps[X][:, 0:128:16], T.G[:, 2048 * b:2048 * b + 2048:16], T.EK[:, 0:8], True, True, Gk(b) + ["EK"], X)
-        for k in CH[c]:
-            mm(ps[X][:, k:128:16], T.VM[:, h + 128 * k:h + 128 * k + 128], ones, True, True, [("VM", b % 2, k), "EK"], X)
-
-    def square(b):
-        i = b % 2
-        E("s", lambda e: e.activation(T["SQ%d" % i][:, 1:129], T.wT[:, 128 * i:128 * i + 128], F.Square, bias=120.0, scale=16.0),
-          [("wT", i)], [("SQ", i)])
+            for j, Q in enumerate((T.CQA[:], T.CQB[:])):
+                if b < 3:
+                    mm(ps[X][:, 0:128], tile(b, j), Q, j == 0, False, Wk, X)
+                else:
+                    mm(ps[X][:, 128:256], Q, tile(b, j), j == 0, False, Wk, X)
+            if b < 3:
+                mm(ps[X][:, 0:128:16], g0, T.DKz[:, 1:9], False, False, Gk(b) + ["DKz"], X)
+            else:
+                mm(ps[X][:, 128:256], T.E0[:], g0, False, False, Gk(b) + ["E0"], X)
+        for i, k in enumerate(CH[c]):
+            if b < 3:
+                mm(ps[X][:, k:128:16], vm(b, c, i), T.ON[:], False, k == 12, [("VM", b % 2, k), "ON"], X)
+            else:
+                mm(ps[X][:, 128:256], T.LO[:, 128 * k:128 * k + 128], vm(b, c, i), False, k == 12, [("VM", b % 2, k), ("LO", k)], X)
 
     def vcopy(b):
-        X = 5 + b % 2
-        tt(T["Vt%d" % (b % 2)][:, 1:129], ps[X][:, 0:128], T["SQ%d" % (b % 2)][:, 0:128], A.add, [("SQ", b % 2)], [("Vt", b % 2)], [X])
+        X, h = 5 + b % 2, 128 * (b % 2)
+        cp(T.Vt[:, h:h + 128], ps[X][:, 0:128], (), [("Vt", b % 2)], [X])
 
     def turn(b):
-        X, V, K = 5 + b % 2, T["Vt%d" % (b % 2)], [("Vt", b % 2)]
-        mm(ps[X][:, 128:256], V[:, 1:129], T.ID[:], True, True, K + ["ID"], X)
-        if b == 3:
-            mm(ps[X][:, 256:384], V[:, 1:129], T.ID[:], True, False, K + ["ID"], X)
-            mm(ps[X][:, 256:384], V[:, 0:128], T.NID[:], False, True, K + ["NID"], X)
+        X, h = 5 + b % 2, 128 * (b % 2)
+        mm(ps[X][:, 128:256], T.Vt[:, h:h + 128], T.ID[:], True, True, [("Vt", b % 2), "ID"], X)
 
-    def vs(b):
+    def vs(t, b):
         X, j = 5 + b % 2, 128 * b
-        cp(T.VS[:, j:j + 128], ps[X][:, 128:256], (), [("VS", b)], [X])
+        cp(T["VS_%d" % t][:, j:j + 128], ps[X][:, 128:256], (), [("VS", t, b)], [X])
 
-    def diff(b):
+    def diff(t, b):
         X, j = 5 + b % 2, 128 * b
-        mm(ps[X][:, 256:384], T.DC[:], T.VS[:, j:j + 128], True, True, [("VS", b), "DC"], X)
+        mm(ps[X][:, 256:384], T.DC[:], T["VS_%d" % t][:, j:j + 128], True, True, [("VS", t, b), "DC"], X)
 
     def cracks(b):
-        X, j = 5 + b % 2, 128 * b
-        return [lambda: ts(T.nd[:], ps[X][:, 256:384], -1.0, None, A.mult, None, (), ["nd"], [X]),
-                lambda: tt(T.ad[:], ps[X][:, 256:384], T.nd[:], A.max, ["nd"], ["ad"], [X]),
-                lambda: ts(T.CC[:, j:j + 128], T.ad[:], c1(THR), None, A.is_gt, None, ["ad", ("col", THR)], [("CC", b)])]
+        X, j, C = 5 + b % 2, 128 * b, 1.5 * 2.0 ** 31
+        ts(T.CC[:, j:j + 128], ps[X][:, 256:384], C, C, A.add, A.not_equal, (), [("CC", b)], [X])
 
-    VSk = [("VS", b) for b in range(4)]
+    def count(b):
+        mm(ps[7][:, 0:128], T.BO[:], T.CC[:, 128 * b:128 * b + 128], b == 0, b == 3, [("CC", b), "BO"], 7)
+
     CCk = [("CC", b) for b in range(4)]
     sent = [0]
 
@@ -323,12 +344,14 @@ def rank_program(g, core, T, topo):
         return len(eg)
 
     def g5(t, a, n):
-        cp(T["cU_%d" % t][:, a:a + n], T.Bt[:, 0:DUMP].indirect(T.nx[:, a // 16:(a + n) // 16]), Bk + BM + ["nx"],
+        m = 1 + a // 256
+        cp(T["cU_%d" % t][:, a:a + n], T.Bt[:, 0:MEND + 256 * m].indirect(T.nx[:, a // 16:(a + n) // 16]), Bk + BM[:m] + ["nx"],
            [("cU", t, x) for x in range(a // 128, (a + n) // 128)])
 
     for t in range(ROUNDS):
-        cU, c16, Dn, pU = T["cU_%d" % t], T["c16_%d" % t], T["Dn_%d" % t], T["pU_%d" % t]
+        cU, c16, VS, pU = T["cU_%d" % t], T["c16_%d" % t], T["VS_%d" % t], T["pU_%d" % t]
         C16 = [("c16", t)]
+        VSk = [("VS", t, b) for b in range(4)]
         last = t == ROUNDS - 1
 
         def bdiag(b, k0=1, k1=16):
@@ -337,102 +360,110 @@ def rank_program(g, core, T, topo):
                 mm(ps[X][:, k:128:16], T.GB[:, 2048 * b + k:2048 * b + 2048:16], T.DK[:, 8 * k:8 * k + 8], True, True,
                    keys("GB", 128 * b, 128) + ["DK"], X)
 
-        xg("s", t, 64, 64)
-        xg("v", t, 0, 64)
-        xg("v", t, 128, 32)
-        xg("s", t, 160, 96)
+        def share(q, step):
+            for tb, a, z in (SHARE_V if q == "v" else SHARE_S)[min(t, 1)][step]:
+                (xg if tb == "x" else bg)(q, t, a, z)
+
+        share("s", 0)
+        share("v", 0)
         ediag(0)
-        Z = zone1(0)
+        Z = near(0)
         Z[0]()
         if t:
             g5(t, 256, 256)
         Z[1]()
         send(t, T["rC_%d" % t][:], cU[:, 256:512], [("cU", t, x) for x in range(4)])
-        zone2(0)
-        zone3(0)
-        square(0)
-        xg("s", t, 256, 128)
+        tiles(0)
+        share("v", 1)
         ts(c16[:], cU[:], -2048.0, None, A.add, None, [("cU", t, x) for x in range(4)], C16)
+        share("s", 1)
+        nop = (lambda: 0)
+        pen(0, 0)
+        pen(0, 1)
         for b in range(NB):
-            C, Z, nop = [], [], (lambda: 0)
-            pen(b, 0)
-            pen(b, 1)
-            if b:
-                turn(b - 1)
-                C = cracks(b - 1)
-            sel(b, 0)
-            if b:
-                vs(b - 1)
-                diff(b - 1)
-            sel(b, 1)
-            if t == 0 and b < 2:
-                unpack(2 * b)
-            pen(b, 2)
             if b < 3:
                 ediag(b + 1)
+            if b:
+                sums(b - 1, 3)
+            Z = near(b + 1) if b < 3 else [nop] * 2
+            sel(b, 0)[0]()
+            pen(b, 2)
+            Z[0]()
+            if b:
+                vcopy(b - 1)
+            Z[1]()
             pen(b, 3)
+            if b:
+                turn(b - 1)
+            sel(b, 1)[0]()
             if b < 3:
-                Z = zone1(b + 1)
-                fg, a = (xg, 384) if b == 0 else (bg, 128 * b - 128 if t else 0)
-            C, Z = C or [nop] * 3, Z or [nop] * 2
+                tiles(b + 1)
+            if b:
+                vs(t, b - 1)
+            if b == 1:
+                act(T.cF[:], c16[:], C16, ["cF"], bias=2048.0)
+            if b < 3:
+                share("s", 2 + b)
             sums(b, 0)
-            S = sel(b, 2, True) + sel(b, 3, True)
-            for f in (C[0], S[0], C[1], S[1], C[2], S[2], Z[0], S[3], Z[1], S[4]):
-                f()
-            if b < 3:
-                if t or b != 1:
-                    fg("s", t, a, 64)
-                square(b + 1)
-                if t or b != 1:
-                    fg("s", t, a + 64, 64)
-                zone2(b + 1)
             sums(b, 1)
-            for f in S[5:]:
-                f()
+            if b:
+                diff(t, b - 1)
+            sel(b, 2)[0]()
+            if b:
+                cracks(b - 1)
             if b < 3:
-                zone3(b + 1)
-            if t == 0 and b < 2:
-                unpack(2 * b + 1)
+                pen(b + 1, 0)
+            if b < 2:
+                share("v", 2 + b)
+            if t == 0:
+                for i in UP[b]:
+                    unpack(i)
+            S = sel(b, 3)
+            S[0]()
             sums(b, 2)
-            sums(b, 3)
-            vcopy(b)
-        for b in (2,) if t else (1, 2):
-            bg("s", t, 128 * b, 128)
-        bg("s", t, 384, 64)
-        mm(ps[1][:, 0:256], T.DM[:], T.VS[:, 0:256], True, True, VSk[:2] + ["DM"], 1)
-        turn(3)
-        bdiag(0, 1, 6)
-        vs(3)
-        C = cracks(3)
-        C[0]()
-        cp(Dn[:, 0:256], ps[1][:, 0:256], (), [("Dn", t, 0)], [1])
-        C[1]()
-        mm(ps[0][:, 0:256], T.DM[:], T.VS[:, 256:512], True, True, VSk[2:] + ["DM"], 0)
-        cp(Dn[:, 256:512], ps[0][:, 0:256], (), [("Dn", t, 1)], [0])
-        C[2]()
+            if b < 3:
+                pen(b + 1, 1)
+            if b:
+                count(b - 1)
+            S[1]()
+            S[2]()
+        piece = [512 - VB]
+
+        def filler():
+            bg("v", t, piece[0], piece[0] + VP)
+            piece[0] += VP
+
+        sums(3, 3)
+        filler()
+        vs(t, 3)
+        diff(t, 3)
+        filler()
         for q in range(16):
-            mm(ps[3][:, 256:288], T.LW[:, 128 * q:128 * q + 128], T.VS[:, q::16], q == 0, q == 15, VSk + [("LW", q)], 3)
-        for q in range(16):
-            mm(ps[4][:, 256:288], T.LO[:, 128 * q:128 * q + 128], T.CC[:, q::16], q == 0, q == 15, CCk + [("LO", q)], 4)
-        bg("v", t, 480, 32)
-        ts(T.Hs[:], ps[3][:, 256:288], c1(H0), None, A.add, None, [("col", H0)], ["Hs"], [3])
-        E("v", lambda e: e.tensor_reduce(T.Rr[:], ps[4][:, 256:288], AxisListType.X, A.add), (), ["Rr"], [4])
-        mm(ps[3][:, 320:321], T.BOf[:], T.Rr[:], True, True, ["BOf", "Rr"], 3)
-        send(t, T["rD_%d" % t][:], Dn[:, 256:512], [("Dn", t, 1)])
-        ts(T.na[:], ps[4][:, 256:288], 5.5, float(DUMP), A.is_gt, A.mult, (), ["na"], [4])
-        ts(T.na1[:], ps[4][:, 256:288], 5.5, None, A.is_gt, None, (), ["na1"], [4])
+            if q == 10:
+                cracks(3)
+                count(3)
+                filler()
+                for r in range(16):
+                    mm(ps[4][:, 384:416], T.LO[:, 128 * r:128 * r + 128], T.CC[:, r::16], r == 0, r == 15, CCk + [("LO", r)], 4)
+            mm(ps[3][:, 384:416], T.LW[:, 128 * q:128 * q + 128], VS[:, q::16], q == 0, q == 15, VSk + [("LW", q)], 3)
+        send(t, T["rD_%d" % t][:], VS[:, 256:512], VSk[2:])
+        E("v", lambda e: e.tensor_reduce(T.Ac[:], ps[7][:, 0:128], AxisListType.X, A.add), (), ["Ac"], [7])
+        filler()
+        ts(T.na[:], ps[4][:, 384:416], 5.5, float(DUMP), A.is_gt, A.mult, (), ["na"], [4])
+        ts(T.na1[:], ps[4][:, 384:416], 5.5, None, A.is_gt, None, (), ["na1"], [4])
+        ts(T.i1[:], ps[3][:, 384:416], T.Ac[:], 512.0, A.add, A.mult, ["Ac"], ["i1"], [3])
         ctt("rp", "na", "iL", A.add)
-        ctt("y1", "na1", "mL", A.mult)
-        Ac = ps[3][:, 320:321]
-        ts(T.i1[:], T.Hs[:], Ac, 512.0, A.add, A.mult, ["Hs"], ["i1"], [3])
-        ts(T.x1[:], T.Hs[:], 37.0, Ac, A.mult, A.add, ["Hs"], ["x1"], [3])
         cts("i2", "i1", 3584, None, A.bitwise_and)
-        cts("x2", "x1", 4095, None, A.bitwise_and)
+        ts(T.x1[:], ps[3][:, 384:416], 37.0, T.Ac[:], A.mult, A.add, ["Ac"], ["x1"], [3])
         ctt("pf", "i2", "rp", A.add)
-        ctt("y3", "x2", "y1", A.max)
+        ctt("y1", "na1", "mL", A.mult)
         cp(pU[:], T.pf[:], ["pf"], [("pU", t)])
-        cp(T.nx[:], T.y3[:], ["y3"], ["nx"])
         ne = 3 * send(t, T["rP_%d" % t][:], pU[:, 16:32], [("pU", t)])
+        cts("x2", "x1", 4095, None, A.bitwise_and)
+        cp(T.Xt[:].indirect(pU[:, 0:16]), VS[:, 0:256], [("pU", t)] + VSk[:2], Xk)
+        ctt("y3", "x2", "y1", A.max)
+        bg("v", t, piece[0], 512)
+        cp(T.nx[:], T.y3[:], ["y3"], ["nx"])
 
         def bturn(b):
             s = slice(128 * b, 128 * b + 128)
@@ -443,54 +474,43 @@ def rank_program(g, core, T, topo):
 
         def mend(a, z):
             s = slice(128 * a, 128 * z)
-            tt(T.t2[:, s], ps[MB[a]][:, s], T.CC[:, s], A.mult, [("CC", b) for b in range(a, z)], [("t2", a)], [MB[a]])
-            tt(T.Bt[:, MEND + 128 * a:MEND + 128 * z], T.t2[:, s], ps[7][:, s], A.add, [("t2", a)], [("Bm", a)], [7])
+            p = ps[MB[a]][:, s]
+            return [lambda: tt(p, p, T.CC[:, s], A.mult, [("CC", b) for b in range(a, z)], [("t2", a)], [MB[a]]),
+                    lambda: tt(T.Bt[:, MEND + 128 * a:MEND + 128 * z], p, T.cF[:, s], A.add, [("t2", a), "cF"], [("Bm", a)], [MB[a]])]
 
-        cp(T.Dt[:].indirect(pU[:, 0:16]), Dn[:, 0:256], [("pU", t), ("Dn", t, 0)], Dk)
-        bg("v", t, 448, 32)
-        bdiag(0, 6, 16)
-        for b in range(NB):
-            if b < 3:
-                bdiag(b + 1)
+        bdiag(0)
+        bdiag(1)
+        bturn(0)
+        bturn(1)
+        bg("s", t, SHARE_S[min(t, 1)][4][-1][2], 384)
+        bg("s", t, 384, 512 - VB)
+        for b in (2, 3):
+            bdiag(b)
+        for b in (2, 3):
             bturn(b)
-            if b in (0, 1):
-                act(ps[7][:, 256 * b:256 * b + 256], c16[:, 256 * b:256 * b + 256], C16, (), [7], bias=2048.0)
-        cp(T.Bt[:].indirect(pU[:, 0:16]), cU[:, 0:256], [("pU", t), ("cU", t, 0), ("cU", t, 1)], Bk + BM)
-        mend(0, 2)
         wr[("arr", t)] = ("arr%d" % t, ne)
         rP = T["rP_%d" % t][:]
-        win = T.Bt[:, 0:DUMP]
-        B5 = Bk + BM + ["nx"]
-
-        def rscat(w):
-            if w:
-                cp(T.Dt[:].indirect(rP), T["rD_%d" % t][:], [("arr", t)], Dk)
-            else:
-                cp(T.Bt[:].indirect(rP), T["rC_%d" % t][:], [("arr", t)], Bk + BM)
-
-        rscat(last)
+        M0, M1 = mend(0, 2), mend(2, 4)
+        cp(T.Xt[:].indirect(rP), T["rD_%d" % t][:], [("arr", t)], Xk)
+        M0[0]()
         if last:
-            rscat(False)
-        mend(2, 4)
+            for i in range(4):
+                c = slice(1024 * i, 1024 * i + 1024)
+                DMA("y", T.yx[:, c], T.Xt[:, c], "o%d" % i, Xk)
+        M0[1]()
+        cp(T.Bt[:].indirect(pU[:, 0:16]), cU[:, 0:256], [("pU", t), ("cU", t, 0), ("cU", t, 1)], Bk + BM)
+        cp(T.Bt[:].indirect(rP), T["rC_%d" % t][:], [("arr", t)], Bk + BM)
         if not last:
-            rscat(True)
             g5(t + 1, 0, 128)
+            M1[0]()
             g5(t + 1, 128, 128)
+            M1[1]()
         else:
+            M1[0]()
+            M1[1]()
             for h in (0, 1):
-                cp(T.ycs[:, h::2], win.indirect(T.nx[:, 16 * h:16 * h + 16]), B5, [("yc", h)])
+                cp(T.ycs[:, h::2], T.Bt[:, 0:DUMP].indirect(T.nx[:, 16 * h:16 * h + 16]), Bk + BM + ["nx"], [("yc", h)])
 
-    for i in range(8):
-        sl = slice(512 * i, 512 * i + 512)
-        X = (1, 2, 3, 4, 6, 1, 2, 3)[i]
-        mm(ps[X][:], T.SX[:], T.Dt[:, sl], True, True, Dk + ["SX"], X)
-        if i < 6:
-            E("s", lambda e: e.activation(T.xin[:, sl], ps[X][:], F.Copy, bias=127.5), (), [("xo", i)], [X])
-        else:
-            ts(T.xin[:, sl], ps[X][:], 127.5, None, A.add, None, (), [("xo", i)], [X])
-        if i % 2:
-            c = slice(512 * (i - 1), 512 * (i + 1))
-            DMA("y", T.yx[:, c], T.xin[:, c], "o%d" % (i // 2), [("xo", i - 1), ("xo", i)])
     DMA("s", T.yc[:], T.ycs[:], "o4", [("yc", 0), ("yc", 1)])
     waits("g", [(s_, 16) for s_ in SEMAPHORES if s_[0] == "o" or (s_[0] == "l" and s_ != "loc")])
     waits("g", [("loc", sent[0])] + [(qsem[q], cnt[q]) for q in qsem])

@@ -9,27 +9,33 @@ MEND = 4096
 DUMP = 4608
 LONG = {"f": "float32", "b": "bfloat16", "h": "float16", "i": "int32", "u": "uint16"}
 SCRATCH = {}
-_spec = """Xt:8704b Bt:8704i pin:2048i ci:512i wi:1i G:8192b GB:8192h VM:4096b R1:256b U:256b Wn:512b Vt:256b
-CC:512b BT:512h cF:512f ycs:512f Ac:1f Hs:32f na:32f na1:32f rp:32f
-i1:32i i2:32i pf:32f x1:32i x2:32i y1:32f y3:32f nx:32u pc:1i ki:1i gi:1i col:32f J:128i Jk:128i Jg:128i JK:128i G8:8i
-I2:2i G2:2i K2:2i GF:2f KF:2f TG:2f K8:16i iL:32f mL:32f iL0:32i mL0:32i u1:128f u2:128f colm:16f TP:128f mA:128f mB:128f
-BO:128b BW:128b ID:128b ID16:128h NID16:128h DKz:136b DK:128h DC:128b E0:128b ON:8b CFA:128b CFB:128b CQA:128b CQB:128b
-PL:2048b LO:2048b LW:2048b"""
+_spec = """Xt:8704b Bt:8704i pin:2048i ci:512i wi:1i G:8192b GB:7680h LB:512u VM:4096b R1:256b U:256b Wn:512b Vt:256b
+CC:512b t2:512f one:128h two:256h ycs:512f BT:512h DK:128h Ac:1f na:32f rp:32f
+i1:64i i2:64i pf:64f y1:32f pc:1i ki:1i gi:1i col:32f J:128i Jk:128i Jg:128i JK:128i G8:8i
+I2:2i G2:2i K2:2i GF:2f KF:2f TG:2f K8:16i iL:32f iL0:32i u1:128f u2:128f colm:16f colk:16f TP:128f mA:128f mB:128f
+BO:128b BW:128b ID:128b ID16:128h NID16:128h DKz:136b DC:128b E0:128b M2:2i QQ:2f J3:128i ON:8b CFA:128b CFB:128b
+CQA:128b CQB:128b CRA:128b CRB:128b PL:2048b LO:2048b LW:2048b"""
 for _t in range(ROUNDS):
-    _spec += " cU_%d:512u c16_%d:512h VS_%d:512b pU_%d:32u rC_%d:256u rD_%d:256b rP_%d:16u" % ((_t,) * 7)
+    _spec += " cU_%d:768u c16_%d:512h VS_%d:512b pU_%d:80u rD_%d:256b" % ((_t,) * 5)
 for _w in _spec.split():
     _n, _d = _w.split(":")
     SCRATCH[_n] = ("sbuf", [128, int(_d[:-1])], LONG[_d[-1]])
 for _t in range(8):
     SCRATCH["ps%d" % _t] = ("psum", [128, 512], "float32")
-SEMAPHORES = "qv qs qt qg loc lci lwt lx0 lx1 lp0 lp1 arr0 arr1 arr2 arr3 o0 o1 o2 o3 o4".split()
-K_, G_, P_, P1, G16, G32, WF, B8, Q38, I0, NI0, K0, HM = range(13)
-VB, VP = 80, 8
-SHARE_V = ((("x", 0, 64), ("x", 128, 160)), (("x", 160, 192),), (), ()), \
-          ((("x", 0, 64), ("x", 128, 160)), (("x", 160, 176),), (("x", 368, 384),), (("x", 496, 512),))
-SHARE_S = ((("x", 64, 128), ("x", 192, 256)), (("x", 256, 352),), (("x", 352, 384), ("x", 384, 512)), (("b", 0, 64),), (("b", 64, 256), ("b", 256, 288))), \
-          ((("x", 64, 128), ("x", 176, 256)), (("x", 256, 352),), (("x", 352, 368), ("x", 384, 448)), (("x", 448, 496), ("b", 0, 48)), (("b", 48, 256), ("b", 256, 288)))
-UP = ((0, 1, 2, 3), (), (), ())
+SEMAPHORES = "qv qs qt qg loc lci lcj lwt lx0 lx1 lp0 lp1 arr0 arr1 arr2 arr3 o0 o1 o4 lc0 lc1 lc2 lc3".split()
+G_, P_, P1, G16, G32, WF, B8, Q38, I0, NI0, HM, K_ = range(12)
+S0, S4 = 48, 296
+SH = ((72, 152, 200, 384, 512, 352, 512, 128, 56, 8),
+      (72, 136, 192, 352, 488, 352, 480, 72, 88, 8),
+      (72, 136, 192, 352, 488, 352, 480, 72, 72, 8))
+
+
+def shares(t):
+    a0, a1, a2, a3, a4, s1, s2, s3, vb, vp = SH[(0, 1, 1, 2)[t]]
+    return {"v": ((("x", a0, 128), ("x", 128, a1)), (("x", a1, a2),), (("x", a3, 384),), (("x", a4, 512),)),
+            "s": ((("x", 0, a0), ("x", a2, 256)), (("x", 256, s1),), (("x", s1, a3), ("x", 384, s2)),
+                  (("x", s2, a4), ("b", 0 if t else S0, s3)), (("b", s3, 256), ("b", 384, 480 - vb), ("b", 256, S4)),
+                  (("b", S4, 384),))}, vb, vp
 
 
 def rank_program(g, core, T, topo):
@@ -124,27 +130,25 @@ def rank_program(g, core, T, topo):
         E("g", lambda e: e.iota(out, pat, base, cm, **kw), (), [key])
 
     Xk, Bk = ["X0", "X1"], [("Bt", i) for i in range(8)]
-    DMA("y", T.ci[:], T.cb[:], "lci", Wk=["ci"])
+    DMA("y", T.ci[:, 0:256], T.cb[:, 0:256], "lci", Wk=[("ci", 0)])
     DMA("s", T.wi[:], T.wt[:], "lwt", Wk=["wi"])
-    for i in range(2):
+    for i in (0, 1):
         DMA("ys"[i], T.Xt[:, 2048 * i:2048 * i + 2048], T.x[:, 2048 * i:2048 * i + 2048], "lx%d" % i, Wk=[Xk[i]])
-    for i in range(2):
-        DMA("ys"[i], T.pin[:, 1024 * i:1024 * i + 1024], T.pk[:, 1024 * i:1024 * i + 1024], "lp%d" % i, Wk=[("pin", i)])
+    DMA("y", T.ci[:, 256:512], T.cb[:, 256:512], "lcj", Wk=[("ci", 1)])
+    DMA("y", T.pin[:, 0:1024], T.pk[:, 0:1024], "lp0", Wk=[("pin", 0)])
 
     iota(T.pc[:], [[0, 1]], 0, 1, "pc")
     iota(T.I2[:], [[55, 2]], 7, 1, "I2")
     iota(T.Jg[:], [[1, 8], [0, 16]], 0, 0, "Jg")
-    for buf, pat, base, cm in (("J", [[1, 128]], 0, 0), ("Jk", [[0, 8], [1, 16]], 0, 0), ("JK", [[1, 16], [16, 8]], 0, 0),
-                               ("K8", [[7, 2], [1, 8]], 0, 0)):
-        iota(T[buf][:], pat, base, cm, buf)
     iota(T.TP[:], [[0, 8], [-256, 2], [32, 8]], 0, 0, ("TP", 0), allow_small_or_imprecise_dtypes=True)
     wr[("TP", 1)] = wr[("TP", 0)]
-    for buf, pat, base, cm in (("G8", [[1, 8]], 0, 0), ("iL0", [[1, 2], [32, 16]], 0, 2), ("mL0", [[16, 32]], MEND, 1)):
+    for buf, pat, base, cm in (("K8", [[7, 2], [1, 8]], 0, 0), ("J", [[1, 128]], 0, 0), ("Jk", [[0, 8], [1, 16]], 0, 0),
+                               ("JK", [[1, 16], [16, 8]], 0, 0), ("G8", [[1, 8]], 0, 0), ("iL0", [[-1, 2], [32, 16]], 1, 2)):
         iota(T[buf][:], pat, base, cm, buf)
     fill(T.U[:], 0.0, [("U", 0), ("U", 1)])
-    fill(T.DKz[:], 0.0, ["DKz"])
-    cts("ki", "pc", 15, None, A.bitwise_and)
+    fill(T.DKz[:], 0.0, ["DKz", "DKz0"])
     cts("gi", "pc", 4, None, A.arith_shift_right)
+    cts("ki", "pc", 15, None, A.bitwise_and)
     colv(P_, "pc", 0.0, None, A.add)
     colv(I0, "pc", 0.0, None, A.is_equal)
     colv(NI0, "pc", 0.0, None, A.not_equal)
@@ -152,31 +156,23 @@ def rank_program(g, core, T, topo):
     colv(Q38, "pc", 64.0, 3808.0, A.is_ge, A.mult)
     colv(P1, "pc", 1.0, None, A.add)
     colv(G_, "gi", 0.0, None, A.add)
-    colv(K0, "ki", 0.0, None, A.is_equal)
-    cts("G2", "I2", 7, None, A.bitwise_and)
+    colv(K_, "ki", 0.0, None, A.add)
     cts("K2", "I2", 3, None, A.arith_shift_right)
+    cts("G2", "I2", 7, None, A.bitwise_and)
     colv(HM, "pc", 64.0, -8.0, A.is_ge, A.mult)
-    colv(G16, "gi", 16.0, None, A.mult)
+    cts("M2", "K2", 3, None, A.bitwise_and)
     cts("GF", "G2", 0.0, None, A.add)
     ts(T.KF[:, 0:1], T.K2[:, 0:1], c1(HM), -1.0, A.add, A.add, ["K2", ("col", HM)], [("KF", 0)])
     ts(T.KF[:, 1:2], T.K2[:, 1:2], c1(HM), c1(NI0), A.add, A.mult, ["K2", ("col", HM), ("col", NI0)], [("KF", 1)])
     cts("TG", "G2", 16.0, 1.0, A.mult, A.add)
+    for j in (0, 1):
+        ts(T.QQ[:, j:j + 1], T.M2[:, j:j + 1], 3.0 * j, c1(Q38), A.not_equal, A.mult, ["M2", ("col", Q38)], [("QQ", j)])
     cts("BO", "Jg", c1(G_), None, A.is_equal, None, [G_])
     cts("mA", "Jg", T.GF[:, 0:1], c1(I0), A.is_equal, A.max, ["GF", I0])
     tt(T.TG[:], T.TG[:], T.KF[:], A.add, ["TG", ("KF", 0), ("KF", 1)], ["TG"])
     cts("mB", "Jg", T.GF[:, 1:2], c1(I0), A.is_equal, A.max, ["GF", I0])
-    cts("ID", "J", c1(P_), None, A.is_equal, None, [P_])
-    cts("u1", "J", c1(P1), None, A.is_equal, None, [P1])
-    cts("u2", "Jk", 0.5, 85.0 / 64, A.is_gt, A.mult)
-    ctt("u1", "ID", "u1", A.subtract)
-    colv(G32, "gi", 32.0, None, A.mult)
-    cts("ID16", "ID", 1.0, None, A.mult)
-    ctt("DC", "u1", "u2", A.mult)
-    cts("NID16", "ID", -1.0, None, A.mult)
-    cts("DK", "JK", c1(P_), None, A.is_equal, None, [P_])
-    for h in (0, 1):
-        cp(T.cU_0[:, 256 * h:256 * h + 256], T.ci[:, h::2], ["ci"], [("cU", 0, 2 * h), ("cU", 0, 2 * h + 1)])
     act(T.TP[0:1, :], T.TP[0:1, :], [("TP", 0)], [("TP", 0)], bias=8.0, scale=1.0 / 16, fn=F.Square)
+    DMA("s", T.pin[:, 1024:2048], T.pk[:, 1024:2048], "lp1", Wk=[("pin", 1)])
     ts(T.TP[64:128, :], T.TP[64:128, :], -1.0, -256.0, A.mult, A.add, [("TP", 1)], [("TP", 1)])
     ts(T.TP[0:1, :], T.TP[0:1, :], -1.0, 68.0, A.mult, A.add, [("TP", 0)], [("TP", 0)])
     fill(T.TP[64:128, 8::16], 32.0, [("TP", 1)])
@@ -185,31 +181,54 @@ def rank_program(g, core, T, topo):
     ts(T.colm[:, 8:9], T.K8[:, 8:9], T.KF[:, 1:2], None, A.is_equal, None, ["K8", ("KF", 1)], [("cm", 1)])
     fill(T.TP[0:1, 8::16], -28.0, [("TP", 0)])
     ts(T.colm[:, 9:16], T.K8[:, 9:16], T.KF[:, 1:2], c1(I0), A.is_equal, A.max, ["K8", ("KF", 1), ("col", I0)], [("cm", 2)])
-    ts(T.DKz[:, 1:64], T.JK[:, 0:63], c1(P_), None, A.is_equal, None, ["JK", ("col", P_)], ["DKz"])
     for o, m in (("CFA", "mA"), ("CFB", "mB")):
         tt(T[o][:], T.TP[:], T[m][:], A.mult, [("TP", 0), ("TP", 1), m], [o])
-    ts(T.DKz[:, 65:130], T.JK[:, 63:128], c1(P_), None, A.is_equal, None, ["JK", ("col", P_)], ["DKz"])
     CM = [("cm", i) for i in range(3)]
     for j in range(16):
         o, i, m = T.PL[:, 128 * j:128 * j + 128], ("CFA", "CFB")[j // 8], T.colm[:, j:j + 1]
-        if j % 2:
-            act(o, T[i][:], [i] + CM, [("PL", j)], scale=m)
-        else:
-            ts(o, T[i][:], m, None, A.mult, None, [i] + CM, [("PL", j)])
+        act(o, T[i][:], [i] + CM, [("PL", j)], scale=m)
+    cts("ID", "J", c1(P_), None, A.is_equal, None, [P_])
+    cts("u1", "J", c1(P1), None, A.is_equal, None, [P1])
+    cts("u2", "Jk", 0.5, 85.0 / 64, A.is_gt, A.mult)
+    ctt("u1", "ID", "u1", A.subtract)
+    colv(G32, "gi", 32.0, None, A.mult)
+    ctt("DC", "u1", "u2", A.mult)
+    act(T.ID16[:], T.ID[:], ["ID"], ["ID16"])
+    act(T.NID16[:], T.ID[:], ["ID"], ["NID16"], scale=-1.0)
+    ts(T.colk[:], T.Jk[:, 0:16], c1(K_), None, A.is_equal, None, ["Jk", ("col", K_)], ["colk"])
+    fill(T.one[0:1, :], 1.0, ["one"])
+    fill(T.two[0:1, :], 2048.0, ["two"])
+
+    def first(x):
+        cp(T.cU_0[:, 128 * x:128 * x + 128], T.ci[:, 256 * (x % 2) + 1 - x // 2:256 * (x % 2) + 256:2], [("ci", x % 2)],
+           [("cU", 0, x)])
+
+    first(0)
+    first(2)
+    ts(T.DKz[:, 1:64], T.JK[:, 0:63], c1(P_), None, A.is_equal, None, ["JK", ("col", P_)], ["DKz"])
+    ts(T.DKz[:, 65:130], T.JK[:, 63:128], c1(P_), None, A.is_equal, None, ["JK", ("col", P_), "DKz0"], ["DKz2"])
+    cts("DK", "JK", c1(P_), None, A.is_equal, None, [P_])
+    ts(T.J3[0:1, :], T.J[0:1, :], 3, None, A.bitwise_and, None, ["J"], ["J3"])
+    ts(T.E0[:], T.ID[:], T.colk[:, 0:1], None, A.mult, None, ["ID", "colk"], ["E0"])
     colv(WF, "wi", 0.0, None, A.add)
     cts("ON", "G8", c1(G_), None, A.is_equal, None, [G_])
-    for o, j, c in (("CQA", 0, 1088.0), ("CQB", 1, 4.0)):
+    for o, j in (("CQA", 0), ("CQB", 1)):
+        cts(o, "J", T.TG[:, j:j + 1], T.QQ[:, j:j + 1], A.is_equal, A.mult, ["TG", ("QQ", j)])
+    for o, j in (("CRA", 0), ("CRB", 1)):
         cts(o, "J", T.TG[:, j:j + 1], c1(Q38), A.is_equal, A.mult, ["TG", Q38])
     cts("BW", "BO", c1(WF), None, A.mult, None, [WF])
-    for o, j, c in (("CQA", 0, 1088.0), ("CQB", 1, 4.0)):
-        ts(T[o][0:1, :], T.Jk[0:1, :], 0.5, c, A.is_gt, A.mult, ["Jk"], [o])
-    for o, i in (("LO", "BO"), ("LW", "BW")):
-        for q in range(16):
+    for o, c, i in (("CQA", 1088.0, "J3"), ("CQB", 4.0, "J3"), ("CRA", 1088.0, "Jk"), ("CRB", 4.0, "Jk")):
+        ts(T[o][0:1, :], T[i][0:1, :], 0.5, c, A.is_gt, A.mult, [i], [o])
+
+    def picks(o, i, q0=0):
+        for q in range(q0, 16):
             E("g", lambda e: e.affine_select(T[o][:, 128 * q:128 * q + 128], T[i][:], [[0, 8], [1, 16]], A.is_equal, 0.0, -q, 0),
               [i], [(o, q)])
+
+    iota(T.Bt[:, MEND:DUMP], [[0, 512]], 0, 0, ("Bm", 0))
+    wr[("Bm", 2)] = wr[("Bm", 0)]
+    picks("LO", "BO")
     cts("iL", "iL0", c1(G32), None, A.subtract, None, [G32])
-    cts("mL", "mL0", c1(G16), None, A.subtract, None, [G16])
-    ts(T.E0[:], T.LO[:, 0:128], c1(K0), None, A.mult, None, [("LO", 0), ("col", K0)], ["E0"])
 
     def unpack(i):
         s, n = i // 2, 1024 * (i // 2) + 512 * (i % 2)
@@ -225,9 +244,9 @@ def rank_program(g, core, T, topo):
     def gath(q, dst, win, t, a, n, R, Wk, bias=0.0):
         if not n:
             return
-        w = win.indirect(T["cU_%d" % t][:, a:a + n])
+        w = win.indirect(T.LB[:, 32 + a:32 + a + n] if bias else T["cU_%d" % t][:, a:a + n])
         out = dst[:, 16 * a:16 * (a + n)]
-        R = R + [("cU", t, x) for x in range(a // 128, (a + n + 127) // 128)]
+        R = R + (["LB"] if bias else [("cU", t, x) for x in range(a // 128, (a + n + 127) // 128)])
         if q == "s":
             act(out, w, R, Wk, bias=bias)
         elif bias:
@@ -245,68 +264,73 @@ def rank_program(g, core, T, topo):
         return keys("G", 128 * b, 128)
 
     def ediag(b):
-        X = 3 + b % 2
         for k in range(15):
             a, z = (0, 9) if k == 0 else (1 + 8 * k + (k > 7), 9 + 8 * k + (k >= 7))
-            mm(ps[X][:, a:z], T.G[:, 2048 * b + k:2048 * b + 2048:16], T.DKz[:, a:z], True, True, Gk(b) + ["DKz"], X)
+            mm(ps[3][:, a:z], T.G[:, 2048 * b + k:2048 * b + 2048:16], T.DKz[:, a:z], True, True, Gk(b) + ["DKz", "DKz2"], 3)
 
     def near(b):
-        X, h, i = 3 + b % 2, 128 * (b % 2), b % 2
-        C = 1.5 * 2.0 ** 27
-        return [lambda: ts(T.R1[:, h:h + 122], ps[X][:, 0:122], C, C, A.add, A.subtract, (), [("R1", i)], [X]),
-                lambda: tt(T.U[:, h:h + 122], ps[X][:, 0:122], T.R1[:, h:h + 122], A.subtract, [("R1", i)], [("U", i)], [X])]
+        h, i, C = 128 * (b % 2), b % 2, 1.5 * 2.0 ** 27
+        return [lambda: ts(T.R1[:, h:h + 122], ps[3][:, 0:122], C, C, A.add, A.subtract, (), [("R1", i)], [3]),
+                lambda: tt(T.U[:, h:h + 122], ps[3][:, 0:122], T.R1[:, h:h + 122], A.subtract, [("R1", i)], [("U", i)], [3])]
 
     def tiles(b):
-        X, h, i = 3 + b % 2, 128 * (b % 2), b % 2
+        h, i = 128 * (b % 2), b % 2
         for j in (0, 1):
             for p in (0, 64):
-                mm(ps[X][p:p + 64, 128 + 128 * j:256 + 128 * j], T.U[:, h + 64 * j:h + 64 * j + 64], T.ID[:], True, True,
-                   [("U", i), "ID"], X)
-        act(T.Wn[:, 2 * h:2 * h + 256], ps[X][:, 128:384], [("col", B8)], [("Wn", i)], [X], bias=c1(B8), fn=F.Square)
+                mm(ps[3][p:p + 64, 128 + 128 * j:256 + 128 * j], T.U[:, h + 64 * j:h + 64 * j + 64], T.ID[:], True, True,
+                   [("U", i), "ID"], 3)
+        act(T.Wn[:, 2 * h:2 * h + 256], ps[3][:, 128:384], [("col", B8)], [("Wn", i)], [3], bias=c1(B8), fn=F.Square)
 
-    def tile(b, j):
+    def tile(b, j, n=128):
         a = 256 * (b % 2) + 128 * j
-        return T.Wn[:, a:a + 128]
+        return T.Wn[0:n, a:a + 128]
 
     CH = ((1, 5, 9, 13), (2, 6, 10, 14), (3, 7, 11, 15), (4, 8, 12))
 
     def pen(b, c):
-        X = (4 * b + c) % 3
+        X = (0, 1, 2, 4)[c]
         for i, k in enumerate(CH[c]):
+            o = ps[X][:, i:512:4] if c < 3 else ps[X][:, 128 * i:128 * i + 128]
+            relu = c == 3 and b < 3
+            if relu:
+                mm(o, T.ID[:], T.G[:, 2048 * b + k:2048 * b + 2048:16], True, False, Gk(b) + ["ID"], X)
             js = [k - 1] if k < 8 else [7, 8] if k == 8 else [k]
             for j in js:
-                mm(ps[X][:, i:512:4], T.PL[:, 128 * j:128 * j + 128], tile(b, j // 8), j == js[0], j == js[-1],
+                mm(o, T.PL[:, 128 * j:128 * j + 128], tile(b, j // 8), not relu and j == js[0], j == js[-1],
                    [("PL", j), ("Wn", b % 2)], X)
 
     def vm(b, c, i):
         o = 2048 * (b % 2) + 512 * c
-        return T.VM[:, o + i:o + 512:4]
+        return T.VM[:, o + i:o + 512:4] if c < 3 else T.VM[:, o + 128 * i:o + 128 * i + 128]
 
     def sel(b, c):
-        X, o = (4 * b + c) % 3, 2048 * (b % 2) + 512 * c
+        X, o, Wk = (0, 1, 2, 4)[c], 2048 * (b % 2) + 512 * c, [("VM", b % 2, k) for k in CH[c]]
         if c < 3:
-            return [lambda: tt(T.VM[:, o:o + 512], T.G[:, 2048 * b + c + 1:2048 * b + 2048:4], ps[X][:], A.min, Gk(b),
-                               [("VM", b % 2, k) for k in CH[c]], [X])]
-        return [lambda i=i, k=k: tt(vm(b, c, i), T.G[:, 2048 * b + k:2048 * b + 2048:16], ps[X][:, i:512:4], A.min, Gk(b),
-                                    [("VM", b % 2, k)], [X]) for i, k in enumerate(CH[c])]
+            tt(T.VM[:, o:o + 512], T.G[:, 2048 * b + c + 1:2048 * b + 2048:4], ps[X][:], A.min, Gk(b), Wk, [X])
+        elif b == 3:
+            for i, k in enumerate(CH[c]):
+                tt(vm(b, c, i), T.G[:, 2048 * b + k:2048 * b + 2048:16], ps[X][:, 128 * i:128 * i + 128], A.min, Gk(b), [Wk[i]], [X])
+        else:
+            act(T.VM[:, o:o + 384], ps[X][:, 0:384], (), Wk, [X], bias=-256.0, fn=F.Relu)
 
     def sums(b, c):
-        X, g0, Wk = 5 + b % 2, T.G[:, 2048 * b:2048 * b + 2048:16], [("Wn", b % 2), "CQA", "CQB"]
+        X, Wk = 5 + b % 2, [("Wn", b % 2), "CQA", "CQB", "CRA", "CRB"]
         if c == 0:
-            for j, Q in enumerate((T.CQA[:], T.CQB[:])):
+            for j, Q in enumerate((T.CQA[:], T.CQB[:]) if b < 3 else (T.CRA[:], T.CRB[:])):
                 if b < 3:
                     mm(ps[X][:, 0:128], tile(b, j), Q, j == 0, False, Wk, X)
                 else:
                     mm(ps[X][:, 128:256], Q, tile(b, j), j == 0, False, Wk, X)
+            g0 = T.G[:, 2048 * b:2048 * b + 2048:16]
             if b < 3:
                 mm(ps[X][:, 0:128:16], g0, T.DKz[:, 1:9], False, False, Gk(b) + ["DKz"], X)
             else:
                 mm(ps[X][:, 128:256], T.E0[:], g0, False, False, Gk(b) + ["E0"], X)
         for i, k in enumerate(CH[c]):
             if b < 3:
-                mm(ps[X][:, k:128:16], vm(b, c, i), T.ON[:], False, k == 12, [("VM", b % 2, k), "ON"], X)
+                mm(ps[X][:, k:128:16], vm(b, c, i), T.ON[:], False, k == 15, [("VM", b % 2, k), "ON"], X)
             else:
-                mm(ps[X][:, 128:256], T.LO[:, 128 * k:128 * k + 128], vm(b, c, i), False, k == 12, [("VM", b % 2, k), ("LO", k)], X)
+                mm(ps[X][:, 128:256], T.LO[:, 128 * k:128 * k + 128], vm(b, c, i), False, k == 15, [("VM", b % 2, k), ("LO", k)], X)
 
     def vcopy(b):
         X, h = 5 + b % 2, 128 * (b % 2)
@@ -344,96 +368,132 @@ def rank_program(g, core, T, topo):
         return len(eg)
 
     def g5(t, a, n):
-        m = 1 + a // 256
-        cp(T["cU_%d" % t][:, a:a + n], T.Bt[:, 0:MEND + 256 * m].indirect(T.nx[:, a // 16:(a + n) // 16]), Bk + BM[:m] + ["nx"],
-           [("cU", t, x) for x in range(a // 128, (a + n) // 128)])
+        cp(T["cU_%d" % t][:, a:a + n], T.Bt[:, 0:DUMP].indirect(T["pU_%d" % (t - 1)][:, a // 16:(a + n) // 16]),
+           Bk + BM + [("pU", t - 1)], [("cU", t, x) for x in range(a // 128, (a + n) // 128)])
 
+    def nop():
+        return None
+
+    later = None
     for t in range(ROUNDS):
-        cU, c16, VS, pU = T["cU_%d" % t], T["c16_%d" % t], T["VS_%d" % t], T["pU_%d" % t]
+        cU, c16, VS, pU, rD = T["cU_%d" % t], T["c16_%d" % t], T["VS_%d" % t], T["pU_%d" % t], T["rD_%d" % t]
         C16 = [("c16", t)]
         VSk = [("VS", t, b) for b in range(4)]
         last = t == ROUNDS - 1
+        SHR, VB, VP = shares(t)
 
-        def bdiag(b, k0=1, k1=16):
-            X = (2, 6)[b % 2]
-            for k in range(k0, k1):
-                mm(ps[X][:, k:128:16], T.GB[:, 2048 * b + k:2048 * b + 2048:16], T.DK[:, 8 * k:8 * k + 8], True, True,
-                   keys("GB", 128 * b, 128) + ["DK"], X)
+        def bdiag(b, moved=False):
+            Y, n = 1 + b % 2, 128 - 32 * (b == 3)
+            for k in range(1, 16):
+                dk = T.DK[:, 8 * k:8 * k + 8]
+                if moved:
+                    mm(ps[Y][96:128, k:128:16], T.GB[:, 512 * k - 512:512 * k:16], dk, True, True,
+                       keys("GB", 32 * k - 32, 32) + ["DK"], Y)
+                else:
+                    mm(ps[Y][0:n, k:128:16], T.GB[:, 2048 * b + k:2048 * b + 16 * n:16], dk, True, True,
+                       keys("GB", 128 * b, n) + ["DK"], Y)
 
-        def share(q, step):
-            for tb, a, z in (SHARE_V if q == "v" else SHARE_S)[min(t, 1)][step]:
+        def bturn(b):
+            X, Y, c = MB[b], 1 + b % 2, slice(128 * b, 128 * b + 128)
+            act(T.BT[:, c], ps[Y][:, 0:128], (), [("BT", b)], [Y])
+            mm(ps[X][:, c], T.BT[:, c], T.ID16[:], True, False, [("BT", b), "ID16"], X)
+            mm(ps[X][:, c], T.NID16[:], c16[:, c], False, True, C16 + ["NID16"], X)
+
+        def share(q, step, i=0, j=9):
+            for tb, a, z in SHR[q][step][i:j]:
                 (xg if tb == "x" else bg)(q, t, a, z)
 
-        share("s", 0)
-        share("v", 0)
+        piece = [480 - VB]
+
+        def filler():
+            bg("v", t, piece[0], piece[0] + VP)
+            piece[0] += VP
+
+        share("s", 0, 0, 1)
+        if t:
+            g5(t, 128, 128)
+        share("v", 0, 0, 1)
+        if t:
+            later[0]()
+        else:
+            first(1)
+            first(3)
+        share("s", 0, 1)
+        share("v", 0, 1)
+        if t:
+            later[1]()
         ediag(0)
         Z = near(0)
         Z[0]()
         if t:
             g5(t, 256, 256)
         Z[1]()
-        send(t, T["rC_%d" % t][:], cU[:, 256:512], [("cU", t, x) for x in range(4)])
+        if t == 0:
+            picks("LW", "BW")
+        send(t, cU[:, 512:768], cU[:, 0:256], [("cU", t, 0), ("cU", t, 1)])
+        CU = [("cU", t, x) for x in range(4)]
+        prep("y", CU, ["LB"], ())
+        g.sync.dma_start(T.LB[0::16, :], cU[:, 480:512]).then_inc(T.sem["lc%d" % t], 16)
+        for x in range(1, 128, 16):
+            g.sync.dma_start(T.LB[x:x + 15, 32:512], cU[x:x + 15, 0:480]).then_inc(T.sem["lc%d" % t], 16)
+        mark(("lc%d" % t, 144), "y", CU, ["LB"], ())
         tiles(0)
         share("v", 1)
-        ts(c16[:], cU[:], -2048.0, None, A.add, None, [("cU", t, x) for x in range(4)], C16)
         share("s", 1)
-        nop = (lambda: 0)
         pen(0, 0)
         pen(0, 1)
         for b in range(NB):
             if b < 3:
                 ediag(b + 1)
             if b:
-                sums(b - 1, 3)
+                sums(b - 1, 2)
             Z = near(b + 1) if b < 3 else [nop] * 2
-            sel(b, 0)[0]()
+            sel(b, 0)
             pen(b, 2)
             Z[0]()
             if b:
                 vcopy(b - 1)
+            else:
+                ts(c16[:], cU[:, 0:512], -2048.0, None, A.add, None, [("cU", t, x) for x in range(4)], C16)
             Z[1]()
             pen(b, 3)
             if b:
                 turn(b - 1)
-            sel(b, 1)[0]()
+            sel(b, 1)
             if b < 3:
                 tiles(b + 1)
             if b:
                 vs(t, b - 1)
-            if b == 1:
-                act(T.cF[:], c16[:], C16, ["cF"], bias=2048.0)
             if b < 3:
+                sel(b, 3)
                 share("s", 2 + b)
             sums(b, 0)
-            sums(b, 1)
             if b:
                 diff(t, b - 1)
-            sel(b, 2)[0]()
-            if b:
-                cracks(b - 1)
             if b < 3:
                 pen(b + 1, 0)
+            else:
+                sel(b, 3)
+            sums(b, 1)
             if b < 2:
                 share("v", 2 + b)
-            if t == 0:
-                for i in UP[b]:
+            if b == 2:
+                filler()
+            if b:
+                cracks(b - 1)
+            if t == 0 and b == 0:
+                for i in range(4):
                     unpack(i)
-            S = sel(b, 3)
-            S[0]()
-            sums(b, 2)
+                bg("s", t, 0, S0)
+            sel(b, 2)
             if b < 3:
                 pen(b + 1, 1)
-            if b:
-                count(b - 1)
-            S[1]()
-            S[2]()
-        piece = [512 - VB]
-
-        def filler():
-            bg("v", t, piece[0], piece[0] + VP)
-            piece[0] += VP
-
-        sums(3, 3)
+            sums(b, 3)
+            if b == 2:
+                send(t, rD[:], VS[:, 0:256], VSk[:2])
+        sums(3, 2)
+        for b in range(3):
+            count(b)
         filler()
         vs(t, 3)
         diff(t, 3)
@@ -446,71 +506,58 @@ def rank_program(g, core, T, topo):
                 for r in range(16):
                     mm(ps[4][:, 384:416], T.LO[:, 128 * r:128 * r + 128], T.CC[:, r::16], r == 0, r == 15, CCk + [("LO", r)], 4)
             mm(ps[3][:, 384:416], T.LW[:, 128 * q:128 * q + 128], VS[:, q::16], q == 0, q == 15, VSk + [("LW", q)], 3)
-        send(t, T["rD_%d" % t][:], VS[:, 256:512], VSk[2:])
         E("v", lambda e: e.tensor_reduce(T.Ac[:], ps[7][:, 0:128], AxisListType.X, A.add), (), ["Ac"], [7])
         filler()
         ts(T.na[:], ps[4][:, 384:416], 5.5, float(DUMP), A.is_gt, A.mult, (), ["na"], [4])
-        ts(T.na1[:], ps[4][:, 384:416], 5.5, None, A.is_gt, None, (), ["na1"], [4])
-        ts(T.i1[:], ps[3][:, 384:416], T.Ac[:], 512.0, A.add, A.mult, ["Ac"], ["i1"], [3])
+        ts(T.i1[:, 32:64], ps[3][:, 384:416], T.Ac[:], 512.0, A.add, A.mult, ["Ac"], [("i1", 1)], [3])
+        ts(T.i1[:, 0:32], ps[3][:, 384:416], 37.0, T.Ac[:], A.mult, A.add, ["Ac"], [("i1", 0)], [3])
         ctt("rp", "na", "iL", A.add)
-        cts("i2", "i1", 3584, None, A.bitwise_and)
-        ts(T.x1[:], ps[3][:, 384:416], 37.0, T.Ac[:], A.mult, A.add, ["Ac"], ["x1"], [3])
-        ctt("pf", "i2", "rp", A.add)
-        ctt("y1", "na1", "mL", A.mult)
-        cp(pU[:], T.pf[:], ["pf"], [("pU", t)])
-        ne = 3 * send(t, T["rP_%d" % t][:], pU[:, 16:32], [("pU", t)])
-        cts("x2", "x1", 4095, None, A.bitwise_and)
-        cp(T.Xt[:].indirect(pU[:, 0:16]), VS[:, 0:256], [("pU", t)] + VSk[:2], Xk)
-        ctt("y3", "x2", "y1", A.max)
-        bg("v", t, piece[0], 512)
-        cp(T.nx[:], T.y3[:], ["y3"], ["nx"])
-
-        def bturn(b):
-            s = slice(128 * b, 128 * b + 128)
-            act(T.BT[:, s], ps[(2, 6)[b % 2]][:, 0:128], (), [("BT", b)], [(2, 6)[b % 2]])
-            X = MB[b]
-            mm(ps[X][:, s], T.BT[:, s], T.ID16[:], True, False, [("BT", b), "ID16"], X)
-            mm(ps[X][:, s], T.NID16[:], c16[:, s], False, True, C16 + ["NID16"], X)
+        ts(T.i2[:], T.i1[:], 4095, None, A.bitwise_and, None, [("i1", 0), ("i1", 1)], ["i2"])
+        cts("y1", "rp", float(MEND - DUMP), None, A.add)
+        tt(T.pf[:, 32:64], T.i2[:, 32:64], T.rp[:], A.add, ["i2", "rp"], [("pf", 1)])
+        tt(T.pf[:, 0:32], T.i2[:, 0:32], T.y1[:], A.max, ["i2", "y1"], [("pf", 0)])
+        cp(pU[:, 0:64], T.pf[:], [("pf", 0), ("pf", 1)], [("pU", t)])
+        ne = 3 * send(t, pU[:, 64:80], pU[:, 32:48], [("pU", t)])
+        bg("v", t, piece[0] + VP, 480)
+        cp(T.Xt[:].indirect(pU[:, 48:64]), VS[:, 256:512], [("pU", t)] + VSk[2:], Xk)
 
         def mend(a, z):
-            s = slice(128 * a, 128 * z)
-            p = ps[MB[a]][:, s]
-            return [lambda: tt(p, p, T.CC[:, s], A.mult, [("CC", b) for b in range(a, z)], [("t2", a)], [MB[a]]),
-                    lambda: tt(T.Bt[:, MEND + 128 * a:MEND + 128 * z], p, T.cF[:, s], A.add, [("t2", a), "cF"], [("Bm", a)], [MB[a]])]
+            s, X = slice(128 * a, 128 * z), 7 - a // 2
+            return [lambda: tt(T.t2[:, s], ps[MB[a]][:, s], T.CC[:, s], A.mult, [("CC", b) for b in range(a, z)], [("t2", a)], [MB[a]]),
+                    lambda: tt(T.Bt[:, MEND + 1 - a // 2:DUMP:2], T.t2[:, s], ps[X][:, s], A.add, [("t2", a)], [("Bm", a)], [X])]
 
         bdiag(0)
         bdiag(1)
         bturn(0)
         bturn(1)
-        bg("s", t, SHARE_S[min(t, 1)][4][-1][2], 384)
-        bg("s", t, 384, 512 - VB)
-        for b in (2, 3):
-            bdiag(b)
-        for b in (2, 3):
-            bturn(b)
+        share("s", 5)
+        for h, X in ((0, 7), (256, 6)):
+            mm(ps[X][:, h:h + 256], T.ID16[:], c16[:, h:h + 256], True, False, C16 + ["ID16"], X)
+            mm(ps[X][:, h:h + 256], T.one[0:1, :], T.two[0:1, 0:256], False, True, ["one", "two"], X)
         wr[("arr", t)] = ("arr%d" % t, ne)
-        rP = T["rP_%d" % t][:]
-        M0, M1 = mend(0, 2), mend(2, 4)
-        cp(T.Xt[:].indirect(rP), T["rD_%d" % t][:], [("arr", t)], Xk)
+        M0, later = mend(0, 2), mend(2, 4)
         M0[0]()
-        if last:
-            for i in range(4):
-                c = slice(1024 * i, 1024 * i + 1024)
-                DMA("y", T.yx[:, c], T.Xt[:, c], "o%d" % i, Xk)
+        filler()
         M0[1]()
-        cp(T.Bt[:].indirect(pU[:, 0:16]), cU[:, 0:256], [("pU", t), ("cU", t, 0), ("cU", t, 1)], Bk + BM)
-        cp(T.Bt[:].indirect(rP), T["rC_%d" % t][:], [("arr", t)], Bk + BM)
+        bdiag(3)
+        bdiag(2)
+        bdiag(3, True)
+        bturn(2)
+        bturn(3)
+        cp(T.Xt[:].indirect(pU[:, 64:80]), rD[:], [("arr", t)], Xk)
+        if last:
+            for i in (0, 1):
+                DMA("ys"[i], T.yx[:, 2048 * i:2048 * i + 2048], T.Xt[:, 2048 * i:2048 * i + 2048], "o%d" % i, Xk)
+        cp(T.Bt[:].indirect(pU[:, 48:80]), cU[:, 256:768], [("pU", t), ("cU", t, 2), ("cU", t, 3), ("arr", t)], Bk + BM)
         if not last:
             g5(t + 1, 0, 128)
-            M1[0]()
-            g5(t + 1, 128, 128)
-            M1[1]()
         else:
-            M1[0]()
-            M1[1]()
-            for h in (0, 1):
-                cp(T.ycs[:, h::2], T.Bt[:, 0:DUMP].indirect(T.nx[:, 16 * h:16 * h + 16]), Bk + BM + ["nx"], [("yc", h)])
+            later[0]()
+            later[1]()
+            act(T.ycs[:, 1::2], T.Bt[:, 0:DUMP].indirect(pU[:, 0:16]), Bk + BM + [("pU", t)], [("yc", 0)])
+            cp(T.ycs[:, 0::2], T.Bt[:, 0:DUMP].indirect(pU[:, 16:32]), Bk + BM + [("pU", t)], [("yc", 1)])
 
-    DMA("s", T.yc[:], T.ycs[:], "o4", [("yc", 0), ("yc", 1)])
-    waits("g", [(s_, 16) for s_ in SEMAPHORES if s_[0] == "o" or (s_[0] == "l" and s_ != "loc")])
+    DMA("y", T.yc[:], T.ycs[:], "o4", [("yc", 0), ("yc", 1)])
+    waits("g", [(s_, 16) for s_ in SEMAPHORES if s_[0] == "o" or (s_[0] == "l" and s_ != "loc")] +
+          [("lc%d" % t, 144) for t in range(ROUNDS)])
     waits("g", [("loc", sent[0])] + [(qsem[q], cnt[q]) for q in qsem])

from concourse.mybir import dt, AluOpType, AxisListType, ActivationFunctionType

A = AluOpType
F = ActivationFunctionType
ROUNDS = 4
NB = 4
W = 4096
MEND = 4096
DUMP = 4608
LONG = {"f": "float32", "b": "bfloat16", "h": "float16", "i": "int32", "u": "uint16"}
SCRATCH = {}
_spec = """Xt:8704b Bt:8704i pin:2048i ci:512i wi:1i G:8192b GB:7680h LB:512u VM:4096b R1:256b U:256b Wn:512b Vt:256b
CC:512b t2:512f one:128h two:256h ycs:512f BT:512h DK:128h Ac:1f na:32f rp:32f
i1:64i i2:64i pf:64f y1:32f pc:1i ki:1i gi:1i col:32f J:128i Jk:128i Jg:128i JK:128i G8:8i
I2:2i G2:2i K2:2i GF:2f KF:2f TG:2f K8:16i iL:32f iL0:32i u1:128f u2:128f colm:16f colk:16f TP:128f mA:128f mB:128f
BO:128b BW:128b ID:128b ID16:128h NID16:128h DKz:136b DC:128b E0:128b M2:2i QQ:2f J3:128i ON:8b CFA:128b CFB:128b
CQA:128b CQB:128b CRA:128b CRB:128b PL:2048b LO:2048b LW:2048b"""
for _t in range(ROUNDS):
    _spec += " cU_%d:768u c16_%d:512h VS_%d:512b pU_%d:80u rD_%d:256b" % ((_t,) * 5)
for _w in _spec.split():
    _n, _d = _w.split(":")
    SCRATCH[_n] = ("sbuf", [128, int(_d[:-1])], LONG[_d[-1]])
for _t in range(8):
    SCRATCH["ps%d" % _t] = ("psum", [128, 512], "float32")
SEMAPHORES = "qv qs qt qg loc lci lcj lwt lx0 lx1 lp0 lp1 arr0 arr1 arr2 arr3 o0 o1 o4 lc0 lc1 lc2 lc3".split()
G_, P_, P1, G16, G32, WF, B8, Q38, I0, NI0, HM, K_ = range(12)
S0, S4 = 48, 296
SH = ((72, 152, 200, 384, 512, 352, 512, 128, 56, 8),
      (72, 136, 192, 352, 488, 352, 480, 72, 88, 8),
      (72, 136, 192, 352, 488, 352, 480, 72, 72, 8))


def shares(t):
    a0, a1, a2, a3, a4, s1, s2, s3, vb, vp = SH[(0, 1, 1, 2)[t]]
    return {"v": ((("x", a0, 128), ("x", 128, a1)), (("x", a1, a2),), (("x", a3, 384),), (("x", a4, 512),)),
            "s": ((("x", 0, a0), ("x", a2, 256)), (("x", 256, s1),), (("x", s1, a3), ("x", 384, s2)),
                  (("x", s2, a4), ("b", 0 if t else S0, s3)), (("b", s3, 256), ("b", 384, 480 - vb), ("b", 256, S4)),
                  (("b", S4, 384),))}, vb, vp


def rank_program(g, core, T, topo):
    rank = T.rank_of(core)
    if rank is None:
        return
    eng = {"v": g.vector, "s": g.scalar, "t": g.tensor, "g": g, "y": g.sync}
    qsem = {"v": "qv", "s": "qs", "t": "qt", "g": "qg"}
    cnt = {q: 0 for q in eng}
    know = {q: {} for q in eng}
    snap, wr, rd, bank = {}, {}, {}, {}

    def waits(q, deps):
        best = {}
        for s_, n_ in deps:
            best[s_] = max(best.get(s_, 0), n_)
        for s_ in sorted(best, key=lambda z: -best[z]):
            n_ = best[s_]
            if know[q].get(s_, 0) >= n_:
                continue
            eng[q].wait_ge(T.sem[s_], n_)
            for k2, v2 in list(snap.get((s_, n_), {}).items()) + [(s_, n_)]:
                know[q][k2] = max(know[q].get(k2, 0), v2)

    def prep(q, R, Wk, X):
        deps = [wr[k] for k in list(R) + list(Wk) if k in wr]
        for k in Wk:
            deps += list(rd.get(k, {}).items())
        for k in X:
            deps += [d for d in bank.get(k, {}).items() if d[0] != qsem.get(q)]
        waits(q, deps)

    def mark(tok, q, R, Wk, X):
        d = dict(know[q])
        d[tok[0]] = tok[1]
        snap[tok] = d
        for k in R:
            rd.setdefault(k, {})[tok[0]] = tok[1]
        for k in Wk:
            wr[k] = tok
            rd[k] = {}
        for k in X:
            bank.setdefault(k, {})[tok[0]] = tok[1]

    def E(q, call, R=(), Wk=(), X=()):
        prep(q, R, Wk, X)
        cnt[q] += 1
        call(eng[q]).then_inc(T.sem[qsem[q]], 1)
        mark((qsem[q], cnt[q]), q, R, Wk, X)

    def DMA(q, out, in_, sem, R=(), Wk=()):
        prep(q, R, Wk, ())
        eng[q].dma_start(out, in_).then_inc(T.sem[sem], 16)
        mark((sem, 16), q, R, Wk, ())

    ps = [T["ps%d" % i] for i in range(8)]

    def c1(i):
        return T.col[:, i:i + 1]

    def mm(out, l, r, a, b, R, X):
        E("t", lambda e: e.matmul(out, l, r, a, b), R, (), [X])

    def ts(out, i, s1, s2, o1, o2=None, R=(), Wk=(), X=()):
        if o2 is None:
            E("v", lambda e: e.tensor_scalar(out, i, s1, None, o1), R, Wk, X)
        else:
            E("v", lambda e: e.tensor_scalar(out, i, s1, s2, o1, o2), R, Wk, X)

    def tt(out, a, b, op, R=(), Wk=(), X=()):
        E("v", lambda e: e.tensor_tensor(out, a, b, op), R, Wk, X)

    def cp(out, i, R=(), Wk=(), X=()):
        E("v", lambda e: e.tensor_copy(out, i), R, Wk, X)

    def act(out, i, R=(), Wk=(), X=(), bias=0.0, scale=1.0, fn=F.Identity):
        E("s", lambda e: e.activation(out, i, fn, bias=bias, scale=scale), R, Wk, X)

    def fill(ap, c, Wk):
        E("v", lambda e: e.memset(ap, c), (), Wk)

    def cts(o, i, s1, s2, o1, o2=None, cols=()):
        ts(T[o][:], T[i][:], s1, s2, o1, o2, [i] + [("col", c) if isinstance(c, int) else c for c in cols or ()], [o])

    def ctt(o, a, b, op):
        tt(T[o][:], T[a][:], T[b][:], op, [a, b], [o])

    def colv(i, src, s1, s2, o1, o2=None):
        ts(c1(i), T[src][:], s1, s2, o1, o2, [src], [("col", i)])

    def iota(out, pat, base, cm, key, **kw):
        E("g", lambda e: e.iota(out, pat, base, cm, **kw), (), [key])

    Xk, Bk = ["X0", "X1"], [("Bt", i) for i in range(8)]
    DMA("y", T.ci[:, 0:256], T.cb[:, 0:256], "lci", Wk=[("ci", 0)])
    DMA("s", T.wi[:], T.wt[:], "lwt", Wk=["wi"])
    for i in (0, 1):
        DMA("ys"[i], T.Xt[:, 2048 * i:2048 * i + 2048], T.x[:, 2048 * i:2048 * i + 2048], "lx%d" % i, Wk=[Xk[i]])
    DMA("y", T.ci[:, 256:512], T.cb[:, 256:512], "lcj", Wk=[("ci", 1)])
    DMA("y", T.pin[:, 0:1024], T.pk[:, 0:1024], "lp0", Wk=[("pin", 0)])

    iota(T.pc[:], [[0, 1]], 0, 1, "pc")
    iota(T.I2[:], [[55, 2]], 7, 1, "I2")
    iota(T.Jg[:], [[1, 8], [0, 16]], 0, 0, "Jg")
    iota(T.TP[:], [[0, 8], [-256, 2], [32, 8]], 0, 0, ("TP", 0), allow_small_or_imprecise_dtypes=True)
    wr[("TP", 1)] = wr[("TP", 0)]
    for buf, pat, base, cm in (("K8", [[7, 2], [1, 8]], 0, 0), ("J", [[1, 128]], 0, 0), ("Jk", [[0, 8], [1, 16]], 0, 0),
                               ("JK", [[1, 16], [16, 8]], 0, 0), ("G8", [[1, 8]], 0, 0), ("iL0", [[-1, 2], [32, 16]], 1, 2)):
        iota(T[buf][:], pat, base, cm, buf)
    fill(T.U[:], 0.0, [("U", 0), ("U", 1)])
    fill(T.DKz[:], 0.0, ["DKz", "DKz0"])
    cts("gi", "pc", 4, None, A.arith_shift_right)
    cts("ki", "pc", 15, None, A.bitwise_and)
    colv(P_, "pc", 0.0, None, A.add)
    colv(I0, "pc", 0.0, None, A.is_equal)
    colv(NI0, "pc", 0.0, None, A.not_equal)
    colv(B8, "pc", 64.0, 8.0, A.is_lt, A.mult)
    colv(Q38, "pc", 64.0, 3808.0, A.is_ge, A.mult)
    colv(P1, "pc", 1.0, None, A.add)
    colv(G_, "gi", 0.0, None, A.add)
    colv(K_, "ki", 0.0, None, A.add)
    cts("K2", "I2", 3, None, A.arith_shift_right)
    cts("G2", "I2", 7, None, A.bitwise_and)
    colv(HM, "pc", 64.0, -8.0, A.is_ge, A.mult)
    cts("M2", "K2", 3, None, A.bitwise_and)
    cts("GF", "G2", 0.0, None, A.add)
    ts(T.KF[:, 0:1], T.K2[:, 0:1], c1(HM), -1.0, A.add, A.add, ["K2", ("col", HM)], [("KF", 0)])
    ts(T.KF[:, 1:2], T.K2[:, 1:2], c1(HM), c1(NI0), A.add, A.mult, ["K2", ("col", HM), ("col", NI0)], [("KF", 1)])
    cts("TG", "G2", 16.0, 1.0, A.mult, A.add)
    for j in (0, 1):
        ts(T.QQ[:, j:j + 1], T.M2[:, j:j + 1], 3.0 * j, c1(Q38), A.not_equal, A.mult, ["M2", ("col", Q38)], [("QQ", j)])
    cts("BO", "Jg", c1(G_), None, A.is_equal, None, [G_])
    cts("mA", "Jg", T.GF[:, 0:1], c1(I0), A.is_equal, A.max, ["GF", I0])
    tt(T.TG[:], T.TG[:], T.KF[:], A.add, ["TG", ("KF", 0), ("KF", 1)], ["TG"])
    cts("mB", "Jg", T.GF[:, 1:2], c1(I0), A.is_equal, A.max, ["GF", I0])
    act(T.TP[0:1, :], T.TP[0:1, :], [("TP", 0)], [("TP", 0)], bias=8.0, scale=1.0 / 16, fn=F.Square)
    DMA("s", T.pin[:, 1024:2048], T.pk[:, 1024:2048], "lp1", Wk=[("pin", 1)])
    ts(T.TP[64:128, :], T.TP[64:128, :], -1.0, -256.0, A.mult, A.add, [("TP", 1)], [("TP", 1)])
    ts(T.TP[0:1, :], T.TP[0:1, :], -1.0, 68.0, A.mult, A.add, [("TP", 0)], [("TP", 0)])
    fill(T.TP[64:128, 8::16], 32.0, [("TP", 1)])
    ts(T.colm[:, 0:8], T.K8[:, 0:8], T.KF[:, 0:1], c1(I0), A.is_equal, A.max, ["K8", ("KF", 0), ("col", I0)], [("cm", 0)])
    fill(T.TP[0:64, 8::16], 0.0, [("TP", 0)])
    ts(T.colm[:, 8:9], T.K8[:, 8:9], T.KF[:, 1:2], None, A.is_equal, None, ["K8", ("KF", 1)], [("cm", 1)])
    fill(T.TP[0:1, 8::16], -28.0, [("TP", 0)])
    ts(T.colm[:, 9:16], T.K8[:, 9:16], T.KF[:, 1:2], c1(I0), A.is_equal, A.max, ["K8", ("KF", 1), ("col", I0)], [("cm", 2)])
    for o, m in (("CFA", "mA"), ("CFB", "mB")):
        tt(T[o][:], T.TP[:], T[m][:], A.mult, [("TP", 0), ("TP", 1), m], [o])
    CM = [("cm", i) for i in range(3)]
    for j in range(16):
        o, i, m = T.PL[:, 128 * j:128 * j + 128], ("CFA", "CFB")[j // 8], T.colm[:, j:j + 1]
        act(o, T[i][:], [i] + CM, [("PL", j)], scale=m)
    cts("ID", "J", c1(P_), None, A.is_equal, None, [P_])
    cts("u1", "J", c1(P1), None, A.is_equal, None, [P1])
    cts("u2", "Jk", 0.5, 85.0 / 64, A.is_gt, A.mult)
    ctt("u1", "ID", "u1", A.subtract)
    colv(G32, "gi", 32.0, None, A.mult)
    ctt("DC", "u1", "u2", A.mult)
    act(T.ID16[:], T.ID[:], ["ID"], ["ID16"])
    act(T.NID16[:], T.ID[:], ["ID"], ["NID16"], scale=-1.0)
    ts(T.colk[:], T.Jk[:, 0:16], c1(K_), None, A.is_equal, None, ["Jk", ("col", K_)], ["colk"])
    fill(T.one[0:1, :], 1.0, ["one"])
    fill(T.two[0:1, :], 2048.0, ["two"])

    def first(x):
        cp(T.cU_0[:, 128 * x:128 * x + 128], T.ci[:, 256 * (x % 2) + 1 - x // 2:256 * (x % 2) + 256:2], [("ci", x % 2)],
           [("cU", 0, x)])

    first(0)
    first(2)
    ts(T.DKz[:, 1:64], T.JK[:, 0:63], c1(P_), None, A.is_equal, None, ["JK", ("col", P_)], ["DKz"])
    ts(T.DKz[:, 65:130], T.JK[:, 63:128], c1(P_), None, A.is_equal, None, ["JK", ("col", P_), "DKz0"], ["DKz2"])
    cts("DK", "JK", c1(P_), None, A.is_equal, None, [P_])
    ts(T.J3[0:1, :], T.J[0:1, :], 3, None, A.bitwise_and, None, ["J"], ["J3"])
    ts(T.E0[:], T.ID[:], T.colk[:, 0:1], None, A.mult, None, ["ID", "colk"], ["E0"])
    colv(WF, "wi", 0.0, None, A.add)
    cts("ON", "G8", c1(G_), None, A.is_equal, None, [G_])
    for o, j in (("CQA", 0), ("CQB", 1)):
        cts(o, "J", T.TG[:, j:j + 1], T.QQ[:, j:j + 1], A.is_equal, A.mult, ["TG", ("QQ", j)])
    for o, j in (("CRA", 0), ("CRB", 1)):
        cts(o, "J", T.TG[:, j:j + 1], c1(Q38), A.is_equal, A.mult, ["TG", Q38])
    cts("BW", "BO", c1(WF), None, A.mult, None, [WF])
    for o, c, i in (("CQA", 1088.0, "J3"), ("CQB", 4.0, "J3"), ("CRA", 1088.0, "Jk"), ("CRB", 4.0, "Jk")):
        ts(T[o][0:1, :], T[i][0:1, :], 0.5, c, A.is_gt, A.mult, [i], [o])

    def picks(o, i, q0=0):
        for q in range(q0, 16):
            E("g", lambda e: e.affine_select(T[o][:, 128 * q:128 * q + 128], T[i][:], [[0, 8], [1, 16]], A.is_equal, 0.0, -q, 0),
              [i], [(o, q)])

    iota(T.Bt[:, MEND:DUMP], [[0, 512]], 0, 0, ("Bm", 0))
    wr[("Bm", 2)] = wr[("Bm", 0)]
    picks("LO", "BO")
    cts("iL", "iL0", c1(G32), None, A.subtract, None, [G32])

    def unpack(i):
        s, n = i // 2, 1024 * (i // 2) + 512 * (i % 2)
        j = T.pin[:, n:n + 512]
        ts(T.Bt[:, n:n + 512], j, 4095, None, A.bitwise_and, None, [("pin", s)], [("Bt", i)])
        ts(T.Bt[:, 2048 + n:2560 + n], j, 12, None, A.arith_shift_right, None, [("pin", s)], [("Bt", 4 + i)])

    BM, MB = [("Bm", 0), ("Bm", 2)], (5, 5, 0, 0)

    def keys(n, a, m):
        return [(n, x) for x in range(a // 8, (a + m) // 8)]

    def gath(q, dst, win, t, a, n, R, Wk, bias=0.0):
        if not n:
            return
        w = win.indirect(T.LB[:, 32 + a:32 + a + n] if bias else T["cU_%d" % t][:, a:a + n])
        out = dst[:, 16 * a:16 * (a + n)]
        R = R + (["LB"] if bias else [("cU", t, x) for x in range(a // 128, (a + n + 127) // 128)])
        if q == "s":
            act(out, w, R, Wk, bias=bias)
        elif bias:
            ts(out, w, bias, None, A.add, None, R, Wk)
        else:
            cp(out, w, R, Wk)

    def xg(q, t, a, z):
        gath(q, T.G, T.Xt[:, 0:W], t, a, z - a, Xk, keys("G", a, z - a))

    def bg(q, t, a, z):
        gath(q, T.GB, T.Bt[:, 0:W], t, a, z - a, Bk, keys("GB", a, z - a), -2048.0)

    def Gk(b):
        return keys("G", 128 * b, 128)

    def ediag(b):
        for k in range(15):
            a, z = (0, 9) if k == 0 else (1 + 8 * k + (k > 7), 9 + 8 * k + (k >= 7))
            mm(ps[3][:, a:z], T.G[:, 2048 * b + k:2048 * b + 2048:16], T.DKz[:, a:z], True, True, Gk(b) + ["DKz", "DKz2"], 3)

    def near(b):
        h, i, C = 128 * (b % 2), b % 2, 1.5 * 2.0 ** 27
        return [lambda: ts(T.R1[:, h:h + 122], ps[3][:, 0:122], C, C, A.add, A.subtract, (), [("R1", i)], [3]),
                lambda: tt(T.U[:, h:h + 122], ps[3][:, 0:122], T.R1[:, h:h + 122], A.subtract, [("R1", i)], [("U", i)], [3])]

    def tiles(b):
        h, i = 128 * (b % 2), b % 2
        for j in (0, 1):
            for p in (0, 64):
                mm(ps[3][p:p + 64, 128 + 128 * j:256 + 128 * j], T.U[:, h + 64 * j:h + 64 * j + 64], T.ID[:], True, True,
                   [("U", i), "ID"], 3)
        act(T.Wn[:, 2 * h:2 * h + 256], ps[3][:, 128:384], [("col", B8)], [("Wn", i)], [3], bias=c1(B8), fn=F.Square)

    def tile(b, j, n=128):
        a = 256 * (b % 2) + 128 * j
        return T.Wn[0:n, a:a + 128]

    CH = ((1, 5, 9, 13), (2, 6, 10, 14), (3, 7, 11, 15), (4, 8, 12))

    def pen(b, c):
        X = (0, 1, 2, 4)[c]
        for i, k in enumerate(CH[c]):
            o = ps[X][:, i:512:4] if c < 3 else ps[X][:, 128 * i:128 * i + 128]
            relu = c == 3 and b < 3
            if relu:
                mm(o, T.ID[:], T.G[:, 2048 * b + k:2048 * b + 2048:16], True, False, Gk(b) + ["ID"], X)
            js = [k - 1] if k < 8 else [7, 8] if k == 8 else [k]
            for j in js:
                mm(o, T.PL[:, 128 * j:128 * j + 128], tile(b, j // 8), not relu and j == js[0], j == js[-1],
                   [("PL", j), ("Wn", b % 2)], X)

    def vm(b, c, i):
        o = 2048 * (b % 2) + 512 * c
        return T.VM[:, o + i:o + 512:4] if c < 3 else T.VM[:, o + 128 * i:o + 128 * i + 128]

    def sel(b, c):
        X, o, Wk = (0, 1, 2, 4)[c], 2048 * (b % 2) + 512 * c, [("VM", b % 2, k) for k in CH[c]]
        if c < 3:
            tt(T.VM[:, o:o + 512], T.G[:, 2048 * b + c + 1:2048 * b + 2048:4], ps[X][:], A.min, Gk(b), Wk, [X])
        elif b == 3:
            for i, k in enumerate(CH[c]):
                tt(vm(b, c, i), T.G[:, 2048 * b + k:2048 * b + 2048:16], ps[X][:, 128 * i:128 * i + 128], A.min, Gk(b), [Wk[i]], [X])
        else:
            act(T.VM[:, o:o + 384], ps[X][:, 0:384], (), Wk, [X], bias=-256.0, fn=F.Relu)

    def sums(b, c):
        X, Wk = 5 + b % 2, [("Wn", b % 2), "CQA", "CQB", "CRA", "CRB"]
        if c == 0:
            for j, Q in enumerate((T.CQA[:], T.CQB[:]) if b < 3 else (T.CRA[:], T.CRB[:])):
                if b < 3:
                    mm(ps[X][:, 0:128], tile(b, j), Q, j == 0, False, Wk, X)
                else:
                    mm(ps[X][:, 128:256], Q, tile(b, j), j == 0, False, Wk, X)
            g0 = T.G[:, 2048 * b:2048 * b + 2048:16]
            if b < 3:
                mm(ps[X][:, 0:128:16], g0, T.DKz[:, 1:9], False, False, Gk(b) + ["DKz"], X)
            else:
                mm(ps[X][:, 128:256], T.E0[:], g0, False, False, Gk(b) + ["E0"], X)
        for i, k in enumerate(CH[c]):
            if b < 3:
                mm(ps[X][:, k:128:16], vm(b, c, i), T.ON[:], False, k == 15, [("VM", b % 2, k), "ON"], X)
            else:
                mm(ps[X][:, 128:256], T.LO[:, 128 * k:128 * k + 128], vm(b, c, i), False, k == 15, [("VM", b % 2, k), ("LO", k)], X)

    def vcopy(b):
        X, h = 5 + b % 2, 128 * (b % 2)
        cp(T.Vt[:, h:h + 128], ps[X][:, 0:128], (), [("Vt", b % 2)], [X])

    def turn(b):
        X, h = 5 + b % 2, 128 * (b % 2)
        mm(ps[X][:, 128:256], T.Vt[:, h:h + 128], T.ID[:], True, True, [("Vt", b % 2), "ID"], X)

    def vs(t, b):
        X, j = 5 + b % 2, 128 * b
        cp(T["VS_%d" % t][:, j:j + 128], ps[X][:, 128:256], (), [("VS", t, b)], [X])

    def diff(t, b):
        X, j = 5 + b % 2, 128 * b
        mm(ps[X][:, 256:384], T.DC[:], T["VS_%d" % t][:, j:j + 128], True, True, [("VS", t, b), "DC"], X)

    def cracks(b):
        X, j, C = 5 + b % 2, 128 * b, 1.5 * 2.0 ** 31
        ts(T.CC[:, j:j + 128], ps[X][:, 256:384], C, C, A.add, A.not_equal, (), [("CC", b)], [X])

    def count(b):
        mm(ps[7][:, 0:128], T.BO[:], T.CC[:, 128 * b:128 * b + 128], b == 0, b == 3, [("CC", b), "BO"], 7)

    CCk = [("CC", b) for b in range(4)]
    sent = [0]

    def send(t, out, src, R):
        to = T.cores[(rank + 1 + t % 3) % len(T.cores)]
        eg = topo.engines(core, to)[:8]
        rid, pid, _ = topo.addr(to)
        waits("g", [wr[k] for k in R])
        g.remote_dma(out, src, T.sem["arr%d" % t], T.sem.loc, pid, rid, sum(1 << x for x in eg))
        sent[0] += len(eg)
        return len(eg)

    def g5(t, a, n):
        cp(T["cU_%d" % t][:, a:a + n], T.Bt[:, 0:DUMP].indirect(T["pU_%d" % (t - 1)][:, a // 16:(a + n) // 16]),
           Bk + BM + [("pU", t - 1)], [("cU", t, x) for x in range(a // 128, (a + n) // 128)])

    def nop():
        return None

    later = None
    for t in range(ROUNDS):
        cU, c16, VS, pU, rD = T["cU_%d" % t], T["c16_%d" % t], T["VS_%d" % t], T["pU_%d" % t], T["rD_%d" % t]
        C16 = [("c16", t)]
        VSk = [("VS", t, b) for b in range(4)]
        last = t == ROUNDS - 1
        SHR, VB, VP = shares(t)

        def bdiag(b, moved=False):
            Y, n = 1 + b % 2, 128 - 32 * (b == 3)
            for k in range(1, 16):
                dk = T.DK[:, 8 * k:8 * k + 8]
                if moved:
                    mm(ps[Y][96:128, k:128:16], T.GB[:, 512 * k - 512:512 * k:16], dk, True, True,
                       keys("GB", 32 * k - 32, 32) + ["DK"], Y)
                else:
                    mm(ps[Y][0:n, k:128:16], T.GB[:, 2048 * b + k:2048 * b + 16 * n:16], dk, True, True,
                       keys("GB", 128 * b, n) + ["DK"], Y)

        def bturn(b):
            X, Y, c = MB[b], 1 + b % 2, slice(128 * b, 128 * b + 128)
            act(T.BT[:, c], ps[Y][:, 0:128], (), [("BT", b)], [Y])
            mm(ps[X][:, c], T.BT[:, c], T.ID16[:], True, False, [("BT", b), "ID16"], X)
            mm(ps[X][:, c], T.NID16[:], c16[:, c], False, True, C16 + ["NID16"], X)

        def share(q, step, i=0, j=9):
            for tb, a, z in SHR[q][step][i:j]:
                (xg if tb == "x" else bg)(q, t, a, z)

        piece = [480 - VB]

        def filler():
            bg("v", t, piece[0], piece[0] + VP)
            piece[0] += VP

        share("s", 0, 0, 1)
        if t:
            g5(t, 128, 128)
        share("v", 0, 0, 1)
        if t:
            later[0]()
        else:
            first(1)
            first(3)
        share("s", 0, 1)
        share("v", 0, 1)
        if t:
            later[1]()
        ediag(0)
        Z = near(0)
        Z[0]()
        if t:
            g5(t, 256, 256)
        Z[1]()
        if t == 0:
            picks("LW", "BW")
        send(t, cU[:, 512:768], cU[:, 0:256], [("cU", t, 0), ("cU", t, 1)])
        CU = [("cU", t, x) for x in range(4)]
        prep("y", CU, ["LB"], ())
        g.sync.dma_start(T.LB[0::16, :], cU[:, 480:512]).then_inc(T.sem["lc%d" % t], 16)
        for x in range(1, 128, 16):
            g.sync.dma_start(T.LB[x:x + 15, 32:512], cU[x:x + 15, 0:480]).then_inc(T.sem["lc%d" % t], 16)
        mark(("lc%d" % t, 144), "y", CU, ["LB"], ())
        tiles(0)
        share("v", 1)
        share("s", 1)
        pen(0, 0)
        pen(0, 1)
        for b in range(NB):
            if b < 3:
                ediag(b + 1)
            if b:
                sums(b - 1, 2)
            Z = near(b + 1) if b < 3 else [nop] * 2
            sel(b, 0)
            pen(b, 2)
            Z[0]()
            if b:
                vcopy(b - 1)
            else:
                ts(c16[:], cU[:, 0:512], -2048.0, None, A.add, None, [("cU", t, x) for x in range(4)], C16)
            Z[1]()
            pen(b, 3)
            if b:
                turn(b - 1)
            sel(b, 1)
            if b < 3:
                tiles(b + 1)
            if b:
                vs(t, b - 1)
            if b < 3:
                sel(b, 3)
                share("s", 2 + b)
            sums(b, 0)
            if b:
                diff(t, b - 1)
            if b < 3:
                pen(b + 1, 0)
            else:
                sel(b, 3)
            sums(b, 1)
            if b < 2:
                share("v", 2 + b)
            if b == 2:
                filler()
            if b:
                cracks(b - 1)
            if t == 0 and b == 0:
                for i in range(4):
                    unpack(i)
                bg("s", t, 0, S0)
            sel(b, 2)
            if b < 3:
                pen(b + 1, 1)
            sums(b, 3)
            if b == 2:
                send(t, rD[:], VS[:, 0:256], VSk[:2])
        sums(3, 2)
        for b in range(3):
            count(b)
        filler()
        vs(t, 3)
        diff(t, 3)
        filler()
        for q in range(16):
            if q == 10:
                cracks(3)
                count(3)
                filler()
                for r in range(16):
                    mm(ps[4][:, 384:416], T.LO[:, 128 * r:128 * r + 128], T.CC[:, r::16], r == 0, r == 15, CCk + [("LO", r)], 4)
            mm(ps[3][:, 384:416], T.LW[:, 128 * q:128 * q + 128], VS[:, q::16], q == 0, q == 15, VSk + [("LW", q)], 3)
        E("v", lambda e: e.tensor_reduce(T.Ac[:], ps[7][:, 0:128], AxisListType.X, A.add), (), ["Ac"], [7])
        filler()
        ts(T.na[:], ps[4][:, 384:416], 5.5, float(DUMP), A.is_gt, A.mult, (), ["na"], [4])
        ts(T.i1[:, 32:64], ps[3][:, 384:416], T.Ac[:], 512.0, A.add, A.mult, ["Ac"], [("i1", 1)], [3])
        ts(T.i1[:, 0:32], ps[3][:, 384:416], 37.0, T.Ac[:], A.mult, A.add, ["Ac"], [("i1", 0)], [3])
        ctt("rp", "na", "iL", A.add)
        ts(T.i2[:], T.i1[:], 4095, None, A.bitwise_and, None, [("i1", 0), ("i1", 1)], ["i2"])
        cts("y1", "rp", float(MEND - DUMP), None, A.add)
        tt(T.pf[:, 32:64], T.i2[:, 32:64], T.rp[:], A.add, ["i2", "rp"], [("pf", 1)])
        tt(T.pf[:, 0:32], T.i2[:, 0:32], T.y1[:], A.max, ["i2", "y1"], [("pf", 0)])
        cp(pU[:, 0:64], T.pf[:], [("pf", 0), ("pf", 1)], [("pU", t)])
        ne = 3 * send(t, pU[:, 64:80], pU[:, 32:48], [("pU", t)])
        bg("v", t, piece[0] + VP, 480)
        cp(T.Xt[:].indirect(pU[:, 48:64]), VS[:, 256:512], [("pU", t)] + VSk[2:], Xk)

        def mend(a, z):
            s, X = slice(128 * a, 128 * z), 7 - a // 2
            return [lambda: tt(T.t2[:, s], ps[MB[a]][:, s], T.CC[:, s], A.mult, [("CC", b) for b in range(a, z)], [("t2", a)], [MB[a]]),
                    lambda: tt(T.Bt[:, MEND + 1 - a // 2:DUMP:2], T.t2[:, s], ps[X][:, s], A.add, [("t2", a)], [("Bm", a)], [X])]

        bdiag(0)
        bdiag(1)
        bturn(0)
        bturn(1)
        share("s", 5)
        for h, X in ((0, 7), (256, 6)):
            mm(ps[X][:, h:h + 256], T.ID16[:], c16[:, h:h + 256], True, False, C16 + ["ID16"], X)
            mm(ps[X][:, h:h + 256], T.one[0:1, :], T.two[0:1, 0:256], False, True, ["one", "two"], X)
        wr[("arr", t)] = ("arr%d" % t, ne)
        M0, later = mend(0, 2), mend(2, 4)
        M0[0]()
        filler()
        M0[1]()
        bdiag(3)
        bdiag(2)
        bdiag(3, True)
        bturn(2)
        bturn(3)
        cp(T.Xt[:].indirect(pU[:, 64:80]), rD[:], [("arr", t)], Xk)
        if last:
            for i in (0, 1):
                DMA("ys"[i], T.yx[:, 2048 * i:2048 * i + 2048], T.Xt[:, 2048 * i:2048 * i + 2048], "o%d" % i, Xk)
        cp(T.Bt[:].indirect(pU[:, 48:80]), cU[:, 256:768], [("pU", t), ("cU", t, 2), ("cU", t, 3), ("arr", t)], Bk + BM)
        if not last:
            g5(t + 1, 0, 128)
        else:
            later[0]()
            later[1]()
            act(T.ycs[:, 1::2], T.Bt[:, 0:DUMP].indirect(pU[:, 0:16]), Bk + BM + [("pU", t)], [("yc", 0)])
            cp(T.ycs[:, 0::2], T.Bt[:, 0:DUMP].indirect(pU[:, 16:32]), Bk + BM + [("pU", t)], [("yc", 1)])

    DMA("y", T.yc[:], T.ycs[:], "o4", [("yc", 0), ("yc", 1)])
    waits("g", [(s_, 16) for s_ in SEMAPHORES if s_[0] == "o" or (s_[0] == "l" and s_ != "loc")] +
          [("lc%d" % t, 144) for t in range(ROUNDS)])
    waits("g", [("loc", sent[0])] + [(qsem[q], cnt[q]) for q in qsem])
